import numpy as np
import ml_dtypes


def mxq(x, axis, fmt="e4m3"):
    dtype, down = {"e4m3": (ml_dtypes.float8_e4m3fn, 7), "e5m2": (ml_dtypes.float8_e5m2, 14)}[fmt]
    v = np.moveaxis(np.asarray(x, np.float32).astype(ml_dtypes.bfloat16).astype(np.float64), axis, -1)
    blocks = v.reshape(v.shape[:-1] + (-1, 32))
    amax = np.abs(blocks).max(-1, keepdims=True)
    byte = np.maximum(np.where(amax > 0, np.frexp(amax)[1] - 1 + 127, 0) - down, 1)
    scale = np.exp2(byte - 127.0)
    codes = (blocks / scale).astype(np.float32).astype(dtype).astype(np.float64)
    return np.moveaxis((codes * scale).reshape(v.shape), -1, axis)


WIDE = False


def mx_kscale(k):
    if not WIDE:
        return np.ones(k)
    levels = np.array([10, -10, 5, -5, 0])
    if k % 512:
        return np.exp2(np.random.permutation(np.resize(levels, k // 32))).repeat(32)
    a = np.empty((k // 512, 16))
    for p in range(k // 512):
        a[p, :8] = np.random.permutation(np.resize(levels, 8))
        for g in range(8):
            far = levels[np.abs(levels - a[p, g]) >= 10]
            a[p, g + 8] = far[np.random.randint(len(far))]
    return np.exp2(a.ravel()).repeat(32)


BF16 = ml_dtypes.bfloat16


def bf(x):
    return np.asarray(x, np.float32).astype(BF16)


def f64(x):
    return np.asarray(x).astype(np.float64)


E2M1 = np.array([0.0, 0.5, 1.0, 1.5, 2.0, 3.0, 4.0, 6.0, -0.0, -0.5, -1.0, -1.5, -2.0, -3.0, -4.0, -6.0])


def pack_weight(w, fmt):
    k, n = w.shape
    w = f64(bf(w)).reshape(k // 32, 32, n)
    amax = np.abs(w).max(1)
    if fmt == "e4m3":
        byte = np.frexp(amax)[1] - 1 + 127 - 7
    else:
        mant, ex = np.frexp(amax / 6.0)
        byte = np.where(mant > 0.5, ex, ex - 1) + 127
    byte = np.clip(np.where(amax > 0, byte, 1), 1, 254)
    scaled = (w * np.exp2(127.0 - byte)[:, None, :]).reshape(k, n).astype(np.float32)
    by_word = np.ascontiguousarray(scaled.reshape(k // 512, 128, 4, n).transpose(0, 1, 3, 2))
    if fmt == "e4m3":
        words = by_word.astype(ml_dtypes.float8_e4m3fn).view(np.uint8)
    else:
        c = by_word.astype(ml_dtypes.float4_e2m1fn).view(np.uint8) & 0xF
        words = c[..., 0::2] | (c[..., 1::2] << 4)
    return np.ascontiguousarray(words), np.ascontiguousarray(byte.astype(np.uint8).reshape(k // 512, 16, n))


def unpack_weight(words, scales, fmt):
    g, p, n, _ = words.shape
    if fmt == "e4m3":
        vals = np.ascontiguousarray(words).view(ml_dtypes.float8_e4m3fn).astype(np.float64)
    else:
        nib = np.empty((g, p, n, 4), np.uint8)
        nib[..., 0::2] = words & 0xF
        nib[..., 1::2] = words >> 4
        vals = E2M1[nib]
    vals = vals * np.repeat(np.exp2(scales.astype(np.float64) - 127.0), 8, axis=1)[..., None]
    return vals.transpose(0, 1, 3, 2).reshape(g * 512, n)

E4M3FN = np.array([(-1.0 if i & 128 else 1.0) * ((1.0 + (i & 7) / 8.0) * 2.0 ** (((i >> 3) & 15) - 7) if i & 120 else (i & 7) * 2.0 ** -9) for i in range(256)])


def e4m3fn_bytes(y):
    return np.clip(np.asarray(y, np.float64), -448.0, 448.0).astype(np.float32).astype(ml_dtypes.float8_e4m3fn).view(np.uint8)


def e4m3fn_values(b):
    return E4M3FN[b]


B, D, H, P = 512, 1024, 1024, 1024


def tanh_jet(a0, a1, a2):
    h0 = np.tanh(a0)
    s = 1.0 - h0 * h0
    h1 = s * a1
    h2 = s * a2 - 2.0 * h0 * s * (a1 * a1)
    return h0, h1, h2


def draw0():
    s, t = mx_kscale(D), mx_kscale(H)
    x = bf(np.random.standard_normal((B, D)) * s)
    v = bf(np.random.standard_normal((B, D)) * s)
    q = bf(np.random.standard_normal((B, D)) * s)
    w1_words, w1_scales = pack_weight(np.random.standard_normal((D, H)) / np.sqrt(D) / s[:, None], "e4m3")
    b = bf(0.3 * np.random.standard_normal(H))
    g = bf((1.0 + 0.1 * np.random.standard_normal(H)) * t)
    w2_words, w2_scales = pack_weight(np.random.standard_normal((H, P)) / np.sqrt(H) / t[:, None], "e4m3")
    return {"x": x,
            "v": v,
            "q": q,
            "w1_words": w1_words,
            "w1_scales": w1_scales,
            "b": b,
            "g": g,
            "w2_words": w2_words,
            "w2_scales": w2_scales}


def core(x, v, q, w1_words, w1_scales, b, g, w2_words, w2_scales):
    w1q = unpack_weight(w1_words, w1_scales, "e4m3")
    a0 = (mxq(f64(x), 1, "e4m3") @ w1q) + f64(b)
    a1 = mxq(f64(v), 1, "e4m3") @ w1q
    a2 = mxq(f64(q), 1, "e4m3") @ w1q
    h0, h1, h2 = tanh_jet(a0, a1, a2)
    gain = f64(g)
    w2q = unpack_weight(w2_words, w2_scales, "e4m3")
    y0 = mxq(gain * h0, 1, "e4m3") @ w2q
    y1 = mxq(gain * h1, 1, "e4m3") @ w2q
    y2 = mxq(gain * h2, 1, "e4m3") @ w2q
    return y0, y1, y2


def setup_inputs():
    drawn = draw0()
    full = np.asarray(drawn['x']).astype(np.float64)
    scale = (np.abs(full).reshape(4, 128, 8, 128).max(axis=(1, 3)) / 448.0).astype(np.float32)
    given = {}
    for key, value in drawn.items():
        if key == 'x':
            given['x_bytes'] = e4m3fn_bytes(full / np.repeat(np.repeat(scale.astype(np.float64), 128, axis=0), 128, axis=1))
            given['x_scale'] = scale
        else:
            given[key] = value
    return given


def reference(x_bytes, x_scale, v, q, w1_words, w1_scales, b, g, w2_words, w2_scales):
    return core(e4m3fn_values(x_bytes) * np.repeat(np.repeat(x_scale.astype(np.float64), 128, axis=0), 128, axis=1), v, q, w1_words, w1_scales, b, g, w2_words, w2_scales)

@@ -1,0 +1,303 @@
+from contextlib import ExitStack
+
+import concourse.mybir as mybir
+from concourse.masks import make_identity
+
+F32 = mybir.dt.float32
+BF16 = mybir.dt.bfloat16
+I32 = mybir.dt.int32
+U32 = mybir.dt.uint32
+U8 = mybir.dt.uint8
+F8 = mybir.dt.float8_e4m3fn
+FP8X4 = mybir.dt.float8_e4m3fn_x4
+ALU = mybir.AluOpType
+ACT = mybir.ActivationFunctionType
+
+P = 128
+B, D, H, N_OUT = 512, 1024, 1024, 1024
+TILES = B // P
+UNITS = 2 * TILES
+GS_S = 2
+FLOPS = 6 * 2 * B * D * H
+
+
+def tile_taylormodesecondordertanhjet_d2p_kernel(tc, x_bytes, x_scale, v, q, w1_words, w1_scales, b, g, w2_words, w2_scales, out_0, out_1, out_2):
+    nc = tc.nc
+    outs = (out_0, out_1, out_2)
+    with ExitStack() as ctx:
+        keep = ctx.enter_context(tc.tile_pool(name="keep", bufs=1))
+        pin = ctx.enter_context(tc.tile_pool(name="pin", bufs=1))
+        work = ctx.enter_context(tc.tile_pool(name="work", bufs=2))
+        psum = ctx.enter_context(tc.psum_pool(name="psum", bufs=1))
+
+        ident = keep.tile([P, P], F32, name="ident")
+        make_identity(nc, ident[:])
+        xs = keep.tile([P, 32], F32, name="xs")
+        b_raw = keep.tile([P, 2, 4], BF16, name="b_raw")
+        g_raw = keep.tile([P, 2, 4], BF16, name="g_raw")
+        b_col = keep.tile([P, 8], F32, name="b_col")
+        g_col = keep.tile([P, 8], F32, name="g_col")
+        ng_col = keep.tile([P, 8], F32, name="ng_col")
+        x_u8 = keep.tile([P, TILES, D], U8, name="x_u8", align_bytes=64)
+        s1_raw = keep.tile([P, H], U8, name="s1_raw", align_bytes=64)
+        s2 = keep.tile([P, N_OUT], U8, name="s2", align_bytes=64)
+        w1_raw = [keep.tile([P, 2, 512], I32, name="w1_raw%d" % h, align_bytes=64) for h in range(2)]
+        w1_per = [keep.tile([P, 2, 512], I32, name="w1_per%d" % h, align_bytes=64) for h in range(2)]
+        s1_per = [keep.tile([P, 512], U8, name="s1_per%d" % h, align_bytes=64) for h in range(2)]
+        w2 = keep.tile([P, 2, N_OUT], I32, name="w2", align_bytes=64)
+        raw = {}
+        for o in (1, 2):
+            for i in range(TILES):
+                raw[o, i] = pin.tile([P, D], BF16, name="raw%d_%d" % (o, i), align_bytes=64)
+
+        st = {}
+
+        def load_rows(o, i):
+            nc.sync.dma_start(out=raw[o, i][:], in_=(v, q)[o - 1][P * i : P * (i + 1), :])
+
+        def load_w1(h):
+            nc.sync.dma_start(out=w1_raw[h][:], in_=w1_words[:, :, 512 * h : 512 * (h + 1), :].rearrange("g p n t -> p g (n t)").bitcast(I32))
+
+        def load_scales(dst, src, eng):
+            for quad in range(4):
+                eng.dma_start(out=dst[32 * quad : 32 * quad + 8, :].bitcast(I32), in_=src[:, 4 * quad : 4 * quad + 4, :].bitcast(I32))
+
+        def widen(i):
+            st["xw", i] = work.tile([P, D], BF16, name="xw", tag="xw", align_bytes=64)
+            for j in range(8):
+                nc.vector.tensor_scalar(
+                    out=st["xw", i][:, P * j : P * (j + 1)],
+                    in0=x_u8[:, i, P * j : P * (j + 1)].bitcast(F8),
+                    scalar1=xs[:, 8 * i + j : 8 * i + j + 1],
+                    scalar2=None,
+                    op0=ALU.mult,
+                )
+
+        def flip(o, i):
+            rows = st["xw", i] if o == 0 else raw[o, i]
+            words = rows[:].bitcast(F32)
+            tr = psum.tile([P, 4, P], F32, name="tr", tag="ytr", bufs=3)
+            for k in range(2):
+                for u in range(2):
+                    nc.tensor.transpose(tr[:, 2 * k + u, :], words[:, 256 * k + u : 256 * (k + 1) : 2], ident[:])
+            st["tr", o, i] = tr
+
+        def gather(o, i):
+            xg = work.tile([P, 2, P, 4], BF16, name="xg", tag="xg", bufs=3, align_bytes=64)
+            nc.scalar.copy(out=xg[:].rearrange("p k r t -> p (k r t)").bitcast(F32).rearrange("p (k r u) -> p k r u", k=2, u=2), in_=st["tr", o, i][:].rearrange("p (k u) r -> p k r u", u=2))
+            st["xg", o, i] = xg
+
+        def quant_in(o, i):
+            xc = work.tile([P, 256], U32, name="xc%d" % o, tag="xc%d" % o, align_bytes=64)
+            xq = work.tile([P, 256], U8, name="xq%d" % o, tag="xq%d" % o, align_bytes=64)
+            nc.vector.quantize_mx(out=xc[:].bitcast(FP8X4), scales=xq[:], in_=st["xg", o, i][:].rearrange("p k r t -> p (k r t)"))
+            st["xc", o, i] = (xc, xq)
+
+        def stage1(o, n):
+            i, h = n // 2, n % 2
+            xc, xq = st["xc", o, i]
+            a = psum.tile([P, 4, P], F32, name="a%d" % o, tag="a%d" % o, bufs=(1, 2, 2)[o])
+            for t in range(4):
+                for k in range(2):
+                    nc.tensor.matmul_mx(
+                        out=a[:, t, :],
+                        lhsT=w1_per[h][:, k, P * t : P * (t + 1)].bitcast(FP8X4),
+                        lhsT_scale=s1_per[h][4 * k : P, P * t : P * (t + 1)],
+                        rhs=xc[:, P * k : P * (k + 1)].bitcast(FP8X4),
+                        rhs_scale=xq[:, P * k : P * (k + 1)],
+                        start=(k == 0),
+                        stop=(k == 1),
+                    )
+            st["a", o, n] = a
+
+        def tanh(n):
+            h = n % 2
+            tt = work.tile([P, 4, P], F32, name="tt", tag="tt")
+            for t in range(4):
+                nc.scalar.activation(out=tt[:, t, :], in_=st["a", 0, n][:, t, :], func=ACT.Tanh, bias=b_col[:, 4 * h + t : 4 * h + t + 1], scale=1.0)
+            st["tt", n] = tt
+
+        def square_a1(n):
+            c = work.tile([P, 4, P], F32, name="c", tag="c")
+            nc.scalar.activation(out=c[:], in_=st["a", 1, n][:], func=ACT.Square)
+            st["c", n] = c
+
+        def square_t(n):
+            sq = work.tile([P, 4, P], F32, name="sq", tag="sq")
+            nc.scalar.activation(out=sq[:], in_=st["tt", n][:], func=ACT.Square)
+            st["sq", n] = sq
+
+        def slope(n, engine_slots):
+            h = n % 2
+            if ("gs", n) not in st:
+                st["gs", n] = work.tile([P, 4, P], F32, name="gs", tag="gs")
+            gs = st["gs", n]
+            for t in engine_slots:
+                c0 = 4 * h + t
+                if t < GS_S:
+                    nc.scalar.activation(out=gs[:, t, :], in_=st["sq", n][:, t, :], func=ACT.Identity, bias=g_col[:, c0 : c0 + 1], scale=ng_col[:, c0 : c0 + 1])
+                    continue
+                nc.vector.tensor_scalar(out=gs[:, t, :], in0=st["sq", n][:, t, :], scalar1=ng_col[:, c0 : c0 + 1], scalar2=g_col[:, c0 : c0 + 1], op0=ALU.mult, op1=ALU.add)
+
+        def curve(n):
+            w = work.tile([P, 4, P], F32, name="w", tag="w")
+            nc.vector.scalar_tensor_tensor(out=w[:], in0=st["tt", n][:], scalar=-2.0, in1=st["c", n][:], op0=ALU.mult, op1=ALU.mult)
+            st["w", n] = w
+
+        def gh0(n):
+            h = n % 2
+            hq = work.tile([P, 3, P, 4], BF16, name="hq", tag="hq", align_bytes=64)
+            st["hq", n] = hq
+            nc.vector.tensor_tensor(out=hq[:, 0, :, :], in0=st["tt", n][:].rearrange("p t n -> p n t"), in1=g_col[:, 4 * h : 4 * h + 4].unsqueeze(1).to_broadcast([P, P, 4]), op=ALU.mult)
+
+        def gh1(n):
+            nc.vector.tensor_tensor(out=st["hq", n][:, 1, :, :], in0=st["gs", n][:].rearrange("p t n -> p n t"), in1=st["a", 1, n][:].rearrange("p t n -> p n t"), op=ALU.mult)
+
+        def bend(n):
+            e = work.tile([P, P, 4], F32, name="e", tag="e")
+            nc.vector.tensor_tensor(out=e[:], in0=st["w", n][:].rearrange("p t n -> p n t"), in1=st["a", 2, n][:].rearrange("p t n -> p n t"), op=ALU.add)
+            st["e", n] = e
+
+        def gh2(n):
+            nc.vector.tensor_tensor(out=st["hq", n][:, 2, :, :], in0=st["gs", n][:].rearrange("p t n -> p n t"), in1=st["e", n][:], op=ALU.mult)
+
+        def codes(n):
+            st["hc", n] = work.tile([P, 3 * P], U32, name="hc", tag="hc", bufs=4, align_bytes=64)
+            st["hs", n] = work.tile([P, 3 * P], U8, name="hs", tag="hs", bufs=4, align_bytes=64)
+
+        def quant(n, lo, hi):
+            nc.vector.quantize_mx(
+                out=st["hc", n][:, P * lo : P * hi].bitcast(FP8X4),
+                scales=st["hs", n][:, P * lo : P * hi],
+                in_=st["hq", n][:, lo:hi, :, :].rearrange("p o n t -> p (o n t)"),
+            )
+
+        def product(o, i, half):
+            slot = o
+            y = psum.tile([P, 512], F32, name="y", tag="ytr", bufs=3)
+            for k in range(2):
+                n = 2 * i + k
+                nc.tensor.matmul_mx(
+                    out=y[:],
+                    lhsT=st["hc", n][:, P * slot : P * (slot + 1)].bitcast(FP8X4),
+                    lhsT_scale=st["hs", n][:, P * slot : P * (slot + 1)],
+                    rhs=w2[:, k, 512 * half : 512 * (half + 1)].bitcast(FP8X4),
+                    rhs_scale=s2[4 * k : P, 512 * half : 512 * (half + 1)],
+                    start=(k == 0),
+                    stop=(k == 1),
+                )
+            st["y", o, i, half] = y
+
+        def store(o, i, half, on_vector=False):
+            y_sb = work.tile([P, 512], F32, name="y_sb", tag="y_sb", bufs=12)
+            if on_vector:
+                nc.vector.tensor_copy(out=y_sb[:], in_=st["y", o, i, half][:])
+            else:
+                nc.scalar.copy(out=y_sb[:], in_=st["y", o, i, half][:])
+            nc.sync.dma_start(out=outs[o][P * i : P * (i + 1), 512 * half : 512 * (half + 1)], in_=y_sb[:])
+
+        pieces = [(o, half) for o in range(3) for half in range(2)]
+
+        with tc.manual_schedule():
+            nc.vector.memset(s1_raw[:].bitcast(I32), 0)
+            nc.vector.memset(s2[:].bitcast(I32), 0)
+            nc.sync.dma_start(out=x_u8[:, 0, :], in_=x_bytes[0:P, :])
+            nc.scalar.dma_start(out=xs[:], in_=x_scale.rearrange("i j -> (i j)").partition_broadcast(P))
+            load_scales(s1_raw, w1_scales, nc.scalar)
+            load_rows(1, 0)
+            load_w1(0)
+            load_rows(2, 0)
+            load_w1(1)
+            nc.gpsimd.dma_start(out=b_raw[:], in_=b.rearrange("(k p t) -> p k t", k=2, t=4))
+            nc.gpsimd.dma_start(out=g_raw[:], in_=g.rearrange("(k p t) -> p k t", k=2, t=4))
+            nc.sync.dma_start(out=x_u8[:, 1:TILES, :], in_=x_bytes[P:B, :].rearrange("(i p) k -> p i k", p=P))
+            load_rows(1, 1)
+            load_rows(2, 1)
+            nc.sync.dma_start(out=w2[:], in_=w2_words.rearrange("g p n t -> p g (n t)").bitcast(I32))
+            load_scales(s2, w2_scales, nc.sync)
+            for i in (2, 3):
+                load_rows(1, i)
+                load_rows(2, i)
+
+            def permute(h):
+                nc.vector.tensor_copy(out=w1_per[h][:].rearrange("p k (t m) -> p k t m", t=4), in_=w1_raw[h][:].rearrange("p k (m t) -> p k t m", t=4))
+                nc.vector.tensor_copy(out=s1_per[h][:].rearrange("p (t m) -> p t m", t=4), in_=s1_raw[:, 512 * h : 512 * (h + 1)].rearrange("p (m t) -> p t m", t=4))
+
+            widen(0)
+            flip(0, 0)
+            gather(0, 0)
+            permute(0)
+            quant_in(0, 0)
+            flip(1, 0)
+            gather(1, 0)
+            stage1(0, 0)
+            flip(2, 0)
+            gather(2, 0)
+            nc.vector.tensor_copy(out=b_col[:], in_=b_raw[:].rearrange("p k t -> p (k t)"))
+            nc.vector.tensor_copy(out=g_col[:], in_=g_raw[:].rearrange("p k t -> p (k t)"))
+            quant_in(1, 0)
+            nc.vector.tensor_scalar(out=ng_col[:], in0=g_col[:], scalar1=-1.0, scalar2=None, op0=ALU.mult)
+            tanh(0)
+            stage1(1, 0)
+            quant_in(2, 0)
+            square_t(0)
+            square_a1(0)
+            slope(0, range(GS_S))
+            stage1(2, 0)
+            widen(1)
+            permute(1)
+            flip(0, 1)
+            gather(0, 1)
+
+            for n in range(UNITS):
+                nxt = n + 1
+                tile_done = n // 2 - 1
+                todo = pieces[0:3] if n % 2 == 0 else pieces[3:6]
+                prep = n // 2 + 1 if n % 2 == 0 else n // 2 + 2
+
+                def finish(m):
+                    if tile_done >= 0:
+                        o, half = todo[m]
+                        product(o, tile_done, half)
+                        store(o, tile_done, half)
+
+                curve(n)
+                if nxt < UNITS:
+                    stage1(0, nxt)
+                    stage1(1, nxt)
+                    tanh(nxt)
+                if n > 0:
+                    quant(n - 1, 2, 3)
+                codes(n)
+                gh0(n)
+                if n % 2 == 0 and prep < TILES:
+                    flip(1, prep)
+                    flip(2, prep)
+                    gather(1, prep)
+                    gather(2, prep)
+                finish(0)
+                slope(n, range(GS_S, 4))
+                if nxt < UNITS:
+                    square_t(nxt)
+                    square_a1(nxt)
+                    slope(nxt, range(GS_S))
+                    stage1(2, nxt)
+                if nxt == UNITS:
+                    quant(n, 0, 1)
+                bend(n)
+                if n % 2 == 1 and prep < TILES:
+                    widen(prep)
+                    flip(0, prep)
+                    gather(0, prep)
+                finish(1)
+                gh1(n)
+                if n % 2 == 0 and prep < TILES:
+                    for o in range(3):
+                        quant_in(o, prep)
+                gh2(n)
+                finish(2)
+                quant(n, 1 if nxt == UNITS else 0, 2)
+            quant(UNITS - 1, 2, 3)
+            for m, (o, half) in enumerate(pieces):
+                product(o, TILES - 1, half)
+                store(o, TILES - 1, half, on_vector=(m % 2 == 1))

@@ -17,7 +17,8 @@ P = 128
 B, D, H, N_OUT = 512, 1024, 1024, 1024
 TILES = B // P
 UNITS = 2 * TILES
-GS_S = 2
+SLOPE_S = (0, 4, 4, 4, 4, 4, 4, 4)
+GH0_S = (0, 4, 4, 0, 0, 0, 0, 0)
 FLOPS = 6 * 2 * B * D * H
 
 
@@ -43,7 +44,7 @@ def tile_taylormodesecondordertanhjet_d2p_kernel(tc, x_bytes, x_scale, v, q, w1_
         s2 = keep.tile([P, N_OUT], U8, name="s2", align_bytes=64)
         w1_raw = [keep.tile([P, 2, 512], I32, name="w1_raw%d" % h, align_bytes=64) for h in range(2)]
         w1_per = [keep.tile([P, 2, 512], I32, name="w1_per%d" % h, align_bytes=64) for h in range(2)]
-        s1_per = [keep.tile([P, 512], U8, name="s1_per%d" % h, align_bytes=64) for h in range(2)]
+        s1_per = keep.tile([P, 2, 512], U8, name="s1_per", align_bytes=64)
         w2 = keep.tile([P, 2, N_OUT], I32, name="w2", align_bytes=64)
         raw = {}
         for o in (1, 2):
@@ -102,7 +103,7 @@ def tile_taylormodesecondordertanhjet_d2p_kernel(tc, x_bytes, x_scale, v, q, w1_
                     nc.tensor.matmul_mx(
                         out=a[:, t, :],
                         lhsT=w1_per[h][:, k, P * t : P * (t + 1)].bitcast(FP8X4),
-                        lhsT_scale=s1_per[h][4 * k : P, P * t : P * (t + 1)],
+                        lhsT_scale=s1_per[4 * k : P, h, P * t : P * (t + 1)],
                         rhs=xc[:, P * k : P * (k + 1)].bitcast(FP8X4),
                         rhs_scale=xq[:, P * k : P * (k + 1)],
                         start=(k == 0),
@@ -134,7 +135,7 @@ def tile_taylormodesecondordertanhjet_d2p_kernel(tc, x_bytes, x_scale, v, q, w1_
             gs = st["gs", n]
             for t in engine_slots:
                 c0 = 4 * h + t
-                if t < GS_S:
+                if t < SLOPE_S[n]:
                     nc.scalar.activation(out=gs[:, t, :], in_=st["sq", n][:, t, :], func=ACT.Identity, bias=g_col[:, c0 : c0 + 1], scale=ng_col[:, c0 : c0 + 1])
                     continue
                 nc.vector.tensor_scalar(out=gs[:, t, :], in0=st["sq", n][:, t, :], scalar1=ng_col[:, c0 : c0 + 1], scalar2=g_col[:, c0 : c0 + 1], op0=ALU.mult, op1=ALU.add)
@@ -144,22 +145,33 @@ def tile_taylormodesecondordertanhjet_d2p_kernel(tc, x_bytes, x_scale, v, q, w1_
             nc.vector.scalar_tensor_tensor(out=w[:], in0=st["tt", n][:], scalar=-2.0, in1=st["c", n][:], op0=ALU.mult, op1=ALU.mult)
             st["w", n] = w
 
-        def gh0(n):
+        def gh0(n, slots):
             h = n % 2
-            hq = work.tile([P, 3, P, 4], BF16, name="hq", tag="hq", align_bytes=64)
-            st["hq", n] = hq
-            nc.vector.tensor_tensor(out=hq[:, 0, :, :], in0=st["tt", n][:].rearrange("p t n -> p n t"), in1=g_col[:, 4 * h : 4 * h + 4].unsqueeze(1).to_broadcast([P, P, 4]), op=ALU.mult)
+            if ("hb", n) not in st:
+                st["hb", n] = work.tile([P, 3, 4, P], BF16, name="hb", tag="hb", align_bytes=64)
+            for t in slots:
+                gain = g_col[:, 4 * h + t : 4 * h + t + 1]
+                if t < GH0_S[n]:
+                    nc.scalar.activation(out=st["hb", n][:, 0, t, :], in_=st["tt", n][:, t, :], func=ACT.Copy, scale=gain)
+                else:
+                    nc.vector.tensor_scalar(out=st["hb", n][:, 0, t, :], in0=st["tt", n][:, t, :], scalar1=gain, scalar2=None, op0=ALU.mult)
 
         def gh1(n):
-            nc.vector.tensor_tensor(out=st["hq", n][:, 1, :, :], in0=st["gs", n][:].rearrange("p t n -> p n t"), in1=st["a", 1, n][:].rearrange("p t n -> p n t"), op=ALU.mult)
+            nc.vector.tensor_tensor(out=st["hb", n][:, 1, :, :], in0=st["gs", n][:], in1=st["a", 1, n][:], op=ALU.mult)
 
         def bend(n):
-            e = work.tile([P, P, 4], F32, name="e", tag="e")
-            nc.vector.tensor_tensor(out=e[:], in0=st["w", n][:].rearrange("p t n -> p n t"), in1=st["a", 2, n][:].rearrange("p t n -> p n t"), op=ALU.add)
+            e = work.tile([P, 4, P], F32, name="e", tag="e")
+            nc.vector.tensor_tensor(out=e[:], in0=st["w", n][:], in1=st["a", 2, n][:], op=ALU.add)
             st["e", n] = e
 
         def gh2(n):
-            nc.vector.tensor_tensor(out=st["hq", n][:, 2, :, :], in0=st["gs", n][:].rearrange("p t n -> p n t"), in1=st["e", n][:], op=ALU.mult)
+            nc.vector.tensor_tensor(out=st["hb", n][:, 2, :, :], in0=st["gs", n][:], in1=st["e", n][:], op=ALU.mult)
+
+        def weave(n, lo, hi):
+            if ("hq", n) not in st:
+                st["hq", n] = work.tile([P, 3, P, 4], BF16, name="hq", tag="hq", align_bytes=64)
+            s = slice(lo, hi)
+            nc.vector.tensor_copy(out=st["hq", n][:, s, :, :].rearrange("p o (c i) t -> p o c t i", i=4), in_=st["hb", n][:, s, :, :].rearrange("p o t (c i) -> p o c t i", i=4))
 
         def codes(n):
             st["hc", n] = work.tile([P, 3 * P], U32, name="hc", tag="hc", bufs=4, align_bytes=64)
@@ -172,9 +184,9 @@ def tile_taylormodesecondordertanhjet_d2p_kernel(tc, x_bytes, x_scale, v, q, w1_
                 in_=st["hq", n][:, lo:hi, :, :].rearrange("p o n t -> p (o n t)"),
             )
 
-        def product(o, i, half):
+        def product(o, i, half, tag="ytr", bufs=3):
             slot = o
-            y = psum.tile([P, 512], F32, name="y", tag="ytr", bufs=3)
+            y = psum.tile([P, 512], F32, name="y", tag=tag, bufs=bufs)
             for k in range(2):
                 n = 2 * i + k
                 nc.tensor.matmul_mx(
@@ -199,105 +211,133 @@ def tile_taylormodesecondordertanhjet_d2p_kernel(tc, x_bytes, x_scale, v, q, w1_
         pieces = [(o, half) for o in range(3) for half in range(2)]
 
         with tc.manual_schedule():
+            waiting = []
             nc.vector.memset(s1_raw[:].bitcast(I32), 0)
             nc.vector.memset(s2[:].bitcast(I32), 0)
-            nc.sync.dma_start(out=x_u8[:, 0, :], in_=x_bytes[0:P, :])
             nc.scalar.dma_start(out=xs[:], in_=x_scale.rearrange("i j -> (i j)").partition_broadcast(P))
+            nc.sync.dma_start(out=x_u8[:, 0, :], in_=x_bytes[0:P, :])
             load_scales(s1_raw, w1_scales, nc.scalar)
             load_rows(1, 0)
             load_w1(0)
-            load_rows(2, 0)
-            load_w1(1)
             nc.gpsimd.dma_start(out=b_raw[:], in_=b.rearrange("(k p t) -> p k t", k=2, t=4))
             nc.gpsimd.dma_start(out=g_raw[:], in_=g.rearrange("(k p t) -> p k t", k=2, t=4))
-            nc.sync.dma_start(out=x_u8[:, 1:TILES, :], in_=x_bytes[P:B, :].rearrange("(i p) k -> p i k", p=P))
+            load_rows(2, 0)
+            nc.sync.dma_start(out=x_u8[:, 1, :], in_=x_bytes[P : 2 * P, :])
+            load_w1(1)
             load_rows(1, 1)
             load_rows(2, 1)
+            nc.sync.dma_start(out=x_u8[:, 2:TILES, :], in_=x_bytes[2 * P : B, :].rearrange("(i p) k -> p i k", p=P))
             nc.sync.dma_start(out=w2[:], in_=w2_words.rearrange("g p n t -> p g (n t)").bitcast(I32))
             load_scales(s2, w2_scales, nc.sync)
             for i in (2, 3):
                 load_rows(1, i)
                 load_rows(2, i)
 
-            def permute(h):
+            def permute_words(h):
                 nc.vector.tensor_copy(out=w1_per[h][:].rearrange("p k (t m) -> p k t m", t=4), in_=w1_raw[h][:].rearrange("p k (m t) -> p k t m", t=4))
-                nc.vector.tensor_copy(out=s1_per[h][:].rearrange("p (t m) -> p t m", t=4), in_=s1_raw[:, 512 * h : 512 * (h + 1)].rearrange("p (m t) -> p t m", t=4))
 
             widen(0)
             flip(0, 0)
+            nc.vector.tensor_copy(out=s1_per[:].rearrange("p k (t m) -> p k t m", t=4), in_=s1_raw[:].rearrange("p (k m t) -> p k t m", k=2, t=4))
             gather(0, 0)
-            permute(0)
             quant_in(0, 0)
             flip(1, 0)
             gather(1, 0)
+            permute_words(0)
             stage1(0, 0)
-            flip(2, 0)
-            gather(2, 0)
+            quant_in(1, 0)
             nc.vector.tensor_copy(out=b_col[:], in_=b_raw[:].rearrange("p k t -> p (k t)"))
             nc.vector.tensor_copy(out=g_col[:], in_=g_raw[:].rearrange("p k t -> p (k t)"))
-            quant_in(1, 0)
             nc.vector.tensor_scalar(out=ng_col[:], in0=g_col[:], scalar1=-1.0, scalar2=None, op0=ALU.mult)
             tanh(0)
             stage1(1, 0)
-            quant_in(2, 0)
-            square_t(0)
             square_a1(0)
-            slope(0, range(GS_S))
-            stage1(2, 0)
+            flip(2, 0)
             widen(1)
-            permute(1)
             flip(0, 1)
+            gather(2, 0)
+            permute_words(1)
+            square_t(0)
+            quant_in(2, 0)
             gather(0, 1)
+            stage1(2, 0)
+            slope(0, range(SLOPE_S[0]))
+            gh0(0, range(GH0_S[0]))
 
             for n in range(UNITS):
                 nxt = n + 1
-                tile_done = n // 2 - 1
-                todo = pieces[0:3] if n % 2 == 0 else pieces[3:6]
-                prep = n // 2 + 1 if n % 2 == 0 else n // 2 + 2
+                first = n % 2 == 0
+                done = n // 2 - 1
+                ahead = n // 2 + 1
+                late = nxt == UNITS
+                todo = [(o, half) for o, half in (pieces[0:3] if first else pieces[3:6]) if done >= 0]
 
-                def finish(m):
-                    if tile_done >= 0:
-                        o, half = todo[m]
-                        product(o, tile_done, half)
-                        store(o, tile_done, half)
+                def make(m):
+                    if m < len(todo):
+                        product(todo[m][0], done, todo[m][1])
+                        waiting.append((todo[m][0], done, todo[m][1]))
 
+                def drain():
+                    if waiting:
+                        store(*waiting.pop(0))
+
+                codes(n)
                 curve(n)
-                if nxt < UNITS:
+                if not late:
                     stage1(0, nxt)
                     stage1(1, nxt)
+                drain()
+                if not first and ahead < TILES:
+                    quant_in(2, ahead)
+                if n > 0:
+                    quant(n - 1, 0, 2)
+                    weave(n - 1, 2, 3)
+                if not first and ahead + 1 < TILES:
+                    widen(ahead + 1)
+                if not late:
                     tanh(nxt)
+                    square_a1(nxt)
+                make(0)
+                if first and ahead < TILES:
+                    flip(1, ahead)
+                    gather(1, ahead)
+                elif not first and ahead + 1 < TILES:
+                    flip(0, ahead + 1)
+                    gather(0, ahead + 1)
+                drain()
+                gh0(n, range(GH0_S[n], 4))
+                slope(n, range(SLOPE_S[n], 4))
                 if n > 0:
                     quant(n - 1, 2, 3)
-                codes(n)
-                gh0(n)
-                if n % 2 == 0 and prep < TILES:
-                    flip(1, prep)
-                    flip(2, prep)
-                    gather(1, prep)
-                    gather(2, prep)
-                finish(0)
-                slope(n, range(GS_S, 4))
-                if nxt < UNITS:
+                if not late:
                     square_t(nxt)
-                    square_a1(nxt)
-                    slope(nxt, range(GS_S))
                     stage1(2, nxt)
-                if nxt == UNITS:
-                    quant(n, 0, 1)
+                make(1)
+                if first and ahead < TILES:
+                    flip(2, ahead)
+                    gather(2, ahead)
+                    quant_in(0, ahead)
                 bend(n)
-                if n % 2 == 1 and prep < TILES:
-                    widen(prep)
-                    flip(0, prep)
-                    gather(0, prep)
-                finish(1)
+                drain()
+                if not late:
+                    slope(nxt, range(SLOPE_S[nxt]))
+                if late:
+                    weave(n, 0, 1)
                 gh1(n)
-                if n % 2 == 0 and prep < TILES:
-                    for o in range(3):
-                        quant_in(o, prep)
+                make(2)
+                if late:
+                    quant(n, 0, 1)
+                if not late:
+                    gh0(nxt, range(GH0_S[nxt]))
                 gh2(n)
-                finish(2)
-                quant(n, 1 if nxt == UNITS else 0, 2)
-            quant(UNITS - 1, 2, 3)
+                if first and ahead < TILES:
+                    quant_in(1, ahead)
+                weave(n, 1 if late else 0, 2)
+            last = UNITS - 1
+            drain()
+            weave(last, 2, 3)
+            quant(last, 1, 2)
+            quant(last, 2, 3)
             for m, (o, half) in enumerate(pieces):
-                product(o, TILES - 1, half)
+                product(o, TILES - 1, half, *(("a1", 2), ("a2", 2), ("ytr", 3))[o])
                 store(o, TILES - 1, half, on_vector=(m % 2 == 1))

@@ -17,7 +17,8 @@ P = 128
 B, D, H, N_OUT = 512, 1024, 1024, 1024
 TILES = B // P
 UNITS = 2 * TILES
-SLOPE_S = (0, 4, 4, 4, 4, 4, 4, 4)
+SLOPE_S = (0, 4, 4, 2, 2, 2, 2, 2)
+SPLIT = (3, 3, 3)
 GH0_S = (0, 4, 4, 0, 0, 0, 0, 0)
 FLOPS = 6 * 2 * B * D * H
 
@@ -32,11 +33,9 @@ def tile_taylormodesecondordertanhjet_d2p_kernel(tc, x_bytes, x_scale, v, q, w1_
         psum = ctx.enter_context(tc.psum_pool(name="psum", bufs=1))
 
         ident = keep.tile([P, P], F32, name="ident")
-        make_identity(nc, ident[:])
         xs = keep.tile([P, 32], F32, name="xs")
-        b_raw = keep.tile([P, 2, 4], BF16, name="b_raw")
-        g_raw = keep.tile([P, 2, 4], BF16, name="g_raw")
-        b_col = keep.tile([P, 8], F32, name="b_col")
+        b_col = keep.tile([P, 8], BF16, name="b_col")
+        g_raw = keep.tile([P, 8], BF16, name="g_raw")
         g_col = keep.tile([P, 8], F32, name="g_col")
         ng_col = keep.tile([P, 8], F32, name="ng_col")
         x_u8 = keep.tile([P, TILES, D], U8, name="x_u8", align_bytes=64)
@@ -148,7 +147,7 @@ def tile_taylormodesecondordertanhjet_d2p_kernel(tc, x_bytes, x_scale, v, q, w1_
         def gh0(n, slots):
             h = n % 2
             if ("hb", n) not in st:
-                st["hb", n] = work.tile([P, 3, 4, P], BF16, name="hb", tag="hb", align_bytes=64)
+                st["hb", n] = work.tile([P, 2, 4, P], BF16, name="hb", tag="hb", align_bytes=64)
             for t in slots:
                 gain = g_col[:, 4 * h + t : 4 * h + t + 1]
                 if t < GH0_S[n]:
@@ -157,7 +156,8 @@ def tile_taylormodesecondordertanhjet_d2p_kernel(tc, x_bytes, x_scale, v, q, w1_
                     nc.vector.tensor_scalar(out=st["hb", n][:, 0, t, :], in0=st["tt", n][:, t, :], scalar1=gain, scalar2=None, op0=ALU.mult)
 
         def gh1(n):
-            nc.vector.tensor_tensor(out=st["hb", n][:, 1, :, :], in0=st["gs", n][:], in1=st["a", 1, n][:], op=ALU.mult)
+            st["hq", n] = work.tile([P, 3, P, 4], BF16, name="hq", tag="hq", align_bytes=64)
+            nc.vector.tensor_tensor(out=st["hq", n][:, 2, :, :], in0=st["gs", n][:].rearrange("p t n -> p n t"), in1=st["a", 1, n][:].rearrange("p t n -> p n t"), op=ALU.mult)
 
         def bend(n):
             e = work.tile([P, 4, P], F32, name="e", tag="e")
@@ -165,11 +165,9 @@ def tile_taylormodesecondordertanhjet_d2p_kernel(tc, x_bytes, x_scale, v, q, w1_
             st["e", n] = e
 
         def gh2(n):
-            nc.vector.tensor_tensor(out=st["hb", n][:, 2, :, :], in0=st["gs", n][:], in1=st["e", n][:], op=ALU.mult)
+            nc.vector.tensor_tensor(out=st["hb", n][:, 1, :, :], in0=st["gs", n][:], in1=st["e", n][:], op=ALU.mult)
 
         def weave(n, lo, hi):
-            if ("hq", n) not in st:
-                st["hq", n] = work.tile([P, 3, P, 4], BF16, name="hq", tag="hq", align_bytes=64)
             s = slice(lo, hi)
             nc.vector.tensor_copy(out=st["hq", n][:, s, :, :].rearrange("p o (c i) t -> p o c t i", i=4), in_=st["hb", n][:, s, :, :].rearrange("p o t (c i) -> p o c t i", i=4))
 
@@ -184,13 +182,15 @@ def tile_taylormodesecondordertanhjet_d2p_kernel(tc, x_bytes, x_scale, v, q, w1_
                 in_=st["hq", n][:, lo:hi, :, :].rearrange("p o n t -> p (o n t)"),
             )
 
-        def product(o, i, half, tag="ytr", bufs=3):
-            slot = o
-            y = psum.tile([P, 512], F32, name="y", tag=tag, bufs=bufs)
-            for k in range(2):
+        def bank(o, i, half, tag="ytr", bufs=3):
+            st["y", o, i, half] = psum.tile([P, 512], F32, name="y", tag=tag, bufs=bufs)
+
+        def product(o, i, half, passes=(0, 1)):
+            slot = (0, 2, 1)[o]
+            for k in passes:
                 n = 2 * i + k
                 nc.tensor.matmul_mx(
-                    out=y[:],
+                    out=st["y", o, i, half][:],
                     lhsT=st["hc", n][:, P * slot : P * (slot + 1)].bitcast(FP8X4),
                     lhsT_scale=st["hs", n][:, P * slot : P * (slot + 1)],
                     rhs=w2[:, k, 512 * half : 512 * (half + 1)].bitcast(FP8X4),
@@ -198,7 +198,6 @@ def tile_taylormodesecondordertanhjet_d2p_kernel(tc, x_bytes, x_scale, v, q, w1_
                     start=(k == 0),
                     stop=(k == 1),
                 )
-            st["y", o, i, half] = y
 
         def store(o, i, half, on_vector=False):
             y_sb = work.tile([P, 512], F32, name="y_sb", tag="y_sb", bufs=12)
@@ -208,19 +207,22 @@ def tile_taylormodesecondordertanhjet_d2p_kernel(tc, x_bytes, x_scale, v, q, w1_
                 nc.scalar.copy(out=y_sb[:], in_=st["y", o, i, half][:])
             nc.sync.dma_start(out=outs[o][P * i : P * (i + 1), 512 * half : 512 * (half + 1)], in_=y_sb[:])
 
-        pieces = [(o, half) for o in range(3) for half in range(2)]
+        pieces = [(o, half) for o in (1, 0, 2) for half in range(2)]
 
         with tc.manual_schedule():
             waiting = []
             nc.vector.memset(s1_raw[:].bitcast(I32), 0)
             nc.vector.memset(s2[:].bitcast(I32), 0)
+            nc.gpsimd.dma_start(out=b_col[:].rearrange("p (k t) -> p k t", k=2), in_=b.rearrange("(k p t) -> p k t", k=2, t=4))
+            nc.gpsimd.dma_start(out=g_raw[:].rearrange("p (k t) -> p k t", k=2), in_=g.rearrange("(k p t) -> p k t", k=2, t=4))
+            make_identity(nc, ident[:])
+            nc.gpsimd.tensor_copy(out=g_col[:], in_=g_raw[:])
+            nc.gpsimd.tensor_scalar(out=ng_col[:], in0=g_col[:], scalar1=-1.0, scalar2=None, op0=ALU.mult)
+            load_rows(1, 0)
             nc.scalar.dma_start(out=xs[:], in_=x_scale.rearrange("i j -> (i j)").partition_broadcast(P))
             nc.sync.dma_start(out=x_u8[:, 0, :], in_=x_bytes[0:P, :])
             load_scales(s1_raw, w1_scales, nc.scalar)
-            load_rows(1, 0)
             load_w1(0)
-            nc.gpsimd.dma_start(out=b_raw[:], in_=b.rearrange("(k p t) -> p k t", k=2, t=4))
-            nc.gpsimd.dma_start(out=g_raw[:], in_=g.rearrange("(k p t) -> p k t", k=2, t=4))
             load_rows(2, 0)
             nc.sync.dma_start(out=x_u8[:, 1, :], in_=x_bytes[P : 2 * P, :])
             load_w1(1)
@@ -236,28 +238,29 @@ def tile_taylormodesecondordertanhjet_d2p_kernel(tc, x_bytes, x_scale, v, q, w1_
             def permute_words(h):
                 nc.vector.tensor_copy(out=w1_per[h][:].rearrange("p k (t m) -> p k t m", t=4), in_=w1_raw[h][:].rearrange("p k (m t) -> p k t m", t=4))
 
-            widen(0)
-            flip(0, 0)
-            nc.vector.tensor_copy(out=s1_per[:].rearrange("p k (t m) -> p k t m", t=4), in_=s1_raw[:].rearrange("p (k m t) -> p k t m", k=2, t=4))
-            gather(0, 0)
-            quant_in(0, 0)
+            def permute_scales(h):
+                nc.vector.tensor_copy(out=s1_per[:, h, :].rearrange("p (t m) -> p t m", t=4), in_=s1_raw[:, 512 * h : 512 * (h + 1)].rearrange("p (m t) -> p t m", t=4))
+
             flip(1, 0)
+            widen(0)
             gather(1, 0)
-            permute_words(0)
-            stage1(0, 0)
+            flip(0, 0)
             quant_in(1, 0)
-            nc.vector.tensor_copy(out=b_col[:], in_=b_raw[:].rearrange("p k t -> p (k t)"))
-            nc.vector.tensor_copy(out=g_col[:], in_=g_raw[:].rearrange("p k t -> p (k t)"))
-            nc.vector.tensor_scalar(out=ng_col[:], in0=g_col[:], scalar1=-1.0, scalar2=None, op0=ALU.mult)
-            tanh(0)
+            gather(0, 0)
+            permute_words(0)
+            permute_scales(0)
+            quant_in(0, 0)
             stage1(1, 0)
+            stage1(0, 0)
             square_a1(0)
             flip(2, 0)
+            tanh(0)
+            gather(2, 0)
             widen(1)
             flip(0, 1)
-            gather(2, 0)
-            permute_words(1)
             square_t(0)
+            permute_words(1)
+            permute_scales(1)
             quant_in(2, 0)
             gather(0, 1)
             stage1(2, 0)
@@ -270,10 +273,11 @@ def tile_taylormodesecondordertanhjet_d2p_kernel(tc, x_bytes, x_scale, v, q, w1_
                 done = n // 2 - 1
                 ahead = n // 2 + 1
                 late = nxt == UNITS
-                todo = [(o, half) for o, half in (pieces[0:3] if first else pieces[3:6]) if done >= 0]
+                todo = [(o, half) for o, half in (pieces[0:SPLIT[done]] if first else pieces[SPLIT[done]:6]) if done >= 0]
 
                 def make(m):
                     if m < len(todo):
+                        bank(todo[m][0], done, todo[m][1])
                         product(todo[m][0], done, todo[m][1])
                         waiting.append((todo[m][0], done, todo[m][1]))
 
@@ -290,8 +294,7 @@ def tile_taylormodesecondordertanhjet_d2p_kernel(tc, x_bytes, x_scale, v, q, w1_
                 if not first and ahead < TILES:
                     quant_in(2, ahead)
                 if n > 0:
-                    quant(n - 1, 0, 2)
-                    weave(n - 1, 2, 3)
+                    weave(n - 1, 0, 2)
                 if not first and ahead + 1 < TILES:
                     widen(ahead + 1)
                 if not late:
@@ -305,10 +308,15 @@ def tile_taylormodesecondordertanhjet_d2p_kernel(tc, x_bytes, x_scale, v, q, w1_
                     flip(0, ahead + 1)
                     gather(0, ahead + 1)
                 drain()
-                gh0(n, range(GH0_S[n], 4))
                 slope(n, range(SLOPE_S[n], 4))
-                if n > 0:
-                    quant(n - 1, 2, 3)
+                if late:
+                    gh1(n)
+                    quant(n - 1, 0, 2)
+                    gh0(n, range(GH0_S[n], 4))
+                else:
+                    gh0(n, range(GH0_S[n], 4))
+                    if n > 0:
+                        quant(n - 1, 0, 2)
                 if not late:
                     square_t(nxt)
                     stage1(2, nxt)
@@ -321,23 +329,30 @@ def tile_taylormodesecondordertanhjet_d2p_kernel(tc, x_bytes, x_scale, v, q, w1_
                 drain()
                 if not late:
                     slope(nxt, range(SLOPE_S[nxt]))
-                if late:
-                    weave(n, 0, 1)
-                gh1(n)
-                make(2)
-                if late:
-                    quant(n, 0, 1)
                 if not late:
+                    gh1(n)
+                make(2)
+                make(3)
+                drain()
+                if late:
+                    quant(n, 2, 3)
+                    weave(n, 0, 1)
+                else:
                     gh0(nxt, range(GH0_S[nxt]))
                 gh2(n)
                 if first and ahead < TILES:
                     quant_in(1, ahead)
-                weave(n, 1 if late else 0, 2)
+                if not late:
+                    quant(n, 2, 3)
             last = UNITS - 1
+            i = TILES - 1
             drain()
-            weave(last, 2, 3)
+            quant(last, 0, 1)
+            weave(last, 1, 2)
             quant(last, 1, 2)
-            quant(last, 2, 3)
+            for (o, half), tag, bufs in zip(pieces, ("a1", "a2", "a0", "a1", "a2", "ytr"), (2, 2, 1, 2, 2, 3)):
+                bank(o, i, half, tag, bufs)
+                product(o, i, half, (0,))
             for m, (o, half) in enumerate(pieces):
-                product(o, TILES - 1, half, *(("a1", 2), ("a2", 2), ("ytr", 3))[o])
-                store(o, TILES - 1, half, on_vector=(m % 2 == 1))
+                product(o, i, half, (1,))
+                store(o, i, half, on_vector=(m in (3, 5)))

@@ -17,9 +17,266 @@ P = 128
 B, D, H, N_OUT = 512, 1024, 1024, 1024
 TILES = B // P
 UNITS = 2 * TILES
-SLOPE_S = (0, 4, 4, 2, 2, 2, 2, 2)
-SPLIT = (3, 3, 3)
-GH0_S = (0, 4, 4, 0, 0, 0, 0, 0)
+SLOPE_S = (0, 4, 1, 1, 2, 0, 2, 1)
+WIDEN_S = (0, 0, 0, 0)
+Y_V = (0, 0, 0, 0, 0, 0, 0, 0, 0, 0, 0, 0, 0, 0, 0, 0, 0, 0, 0, 0, 1, 0, 0, 0)
+LASTB = (("a1", 2), ("a2", 2), ("a0", 1), ("a1", 2), ("a2", 2), ("ytr", 3))
+PROGRAM = (
+    ('load', 'xs'),
+    ('load', 'x0'),
+    ('load', 'v0'),
+    ('load', 's1'),
+    ('load', 'w10'),
+    ('load', 'x1'),
+    ('load', 'x23'),
+    ('load', 'q0'),
+    ('load', 'w11'),
+    ('load', 'v1'),
+    ('load', 'q1'),
+    ('load', 'w2'),
+    ('load', 's2'),
+    ('load', 'q2'),
+    ('load', 'q3'),
+    ('load', 'v2'),
+    ('load', 'v3'),
+    ('widen', 0),
+    ('flip', 0, 0),
+    ('flip', 1, 0),
+    ('perms', 1),
+    ('perms', 0),
+    ('gather', 0, 0),
+    ('gather', 1, 0),
+    ('permw', 0),
+    ('quant_in', 0, 0),
+    ('quant_in', 1, 0),
+    ('stage1', 0, 0),
+    ('tanh', 0),
+    ('widen', 1),
+    ('widen', 3),
+    ('flip', 0, 1),
+    ('widen', 2),
+    ('sqt', 0),
+    ('flip', 2, 0),
+    ('stage1', 1, 0),
+    ('gather', 0, 1),
+    ('flip', 1, 1),
+    ('permw', 1),
+    ('slopeS', 0),
+    ('gather', 2, 0),
+    ('gh0S', 0),
+    ('gh0V', 0),
+    ('sqa', 0),
+    ('stage1', 0, 1),
+    ('gather', 1, 1),
+    ('quant_in', 0, 1),
+    ('slopeV', 0),
+    ('quant_in', 2, 0),
+    ('stage1', 1, 1),
+    ('tanh', 1),
+    ('curve', 0),
+    ('stage1', 2, 0),
+    ('quant_in', 1, 1),
+    ('stage1', 0, 2),
+    ('gh1', 0),
+    ('flip', 2, 1),
+    ('sqa', 1),
+    ('bend', 0),
+    ('flip', 0, 2),
+    ('sqt', 1),
+    ('stage1', 2, 1),
+    ('tanh', 2),
+    ('curve', 1),
+    ('slopeS', 1),
+    ('gather', 2, 1),
+    ('gather', 0, 2),
+    ('gh2', 0),
+    ('sqt', 2),
+    ('stage1', 1, 2),
+    ('quant', 0, 2, 3),
+    ('gh0S', 2),
+    ('flip', 1, 2),
+    ('gh0V', 2),
+    ('slopeV', 1),
+    ('sqa', 2),
+    ('weave', 0, 0, 2),
+    ('stage1', 0, 3),
+    ('gather', 1, 2),
+    ('bend', 1),
+    ('gh0V', 1),
+    ('gh0S', 1),
+    ('gh1', 1),
+    ('quant_in', 0, 2),
+    ('slopeV', 2),
+    ('quant_in', 2, 1),
+    ('stage1', 1, 3),
+    ('tanh', 3),
+    ('slopeS', 2),
+    ('quant', 0, 0, 2),
+    ('gh2', 1),
+    ('curve', 2),
+    ('stage1', 2, 2),
+    ('weave', 1, 0, 2),
+    ('quant_in', 1, 2),
+    ('stage1', 0, 4),
+    ('gh1', 2),
+    ('flip', 2, 2),
+    ('sqa', 3),
+    ('quant', 1, 2, 3),
+    ('quant', 1, 0, 2),
+    ('bend', 2),
+    ('flip', 0, 3),
+    ('sqt', 3),
+    ('stage1', 2, 3),
+    ('tanh', 4),
+    ('curve', 3),
+    ('slopeS', 3),
+    ('gather', 2, 2),
+    ('whole', 2, 0, 0),
+    ('gather', 0, 3),
+    ('gh2', 2),
+    ('sqt', 4),
+    ('stage1', 1, 4),
+    ('whole', 0, 0, 0),
+    ('quant', 2, 2, 3),
+    ('gh0S', 4),
+    ('store', 2, 0, 0),
+    ('flip', 1, 3),
+    ('gh0V', 4),
+    ('whole', 2, 0, 1),
+    ('store', 0, 0, 0),
+    ('slopeV', 3),
+    ('sqa', 4),
+    ('whole', 1, 0, 1),
+    ('weave', 2, 0, 2),
+    ('stage1', 0, 5),
+    ('gather', 1, 3),
+    ('bend', 3),
+    ('store', 2, 0, 1),
+    ('gh0V', 3),
+    ('gh0S', 3),
+    ('gh1', 3),
+    ('quant_in', 0, 3),
+    ('slopeV', 4),
+    ('quant_in', 2, 2),
+    ('stage1', 1, 5),
+    ('tanh', 5),
+    ('slopeS', 4),
+    ('whole', 1, 0, 0),
+    ('store', 1, 0, 0),
+    ('quant', 2, 0, 2),
+    ('whole', 0, 0, 1),
+    ('gh2', 3),
+    ('curve', 4),
+    ('stage1', 2, 4),
+    ('weave', 3, 0, 2),
+    ('quant_in', 1, 3),
+    ('stage1', 0, 6),
+    ('gh1', 4),
+    ('store', 0, 0, 1),
+    ('flip', 2, 3),
+    ('sqa', 5),
+    ('quant', 3, 2, 3),
+    ('quant', 3, 0, 2),
+    ('bend', 4),
+    ('sqt', 5),
+    ('stage1', 2, 5),
+    ('tanh', 6),
+    ('store', 1, 0, 1),
+    ('curve', 5),
+    ('slopeS', 5),
+    ('gather', 2, 3),
+    ('whole', 2, 1, 0),
+    ('gh2', 4),
+    ('sqt', 6),
+    ('stage1', 1, 6),
+    ('whole', 0, 1, 0),
+    ('quant', 4, 2, 3),
+    ('gh0S', 6),
+    ('store', 2, 1, 0),
+    ('gh0V', 6),
+    ('whole', 2, 1, 1),
+    ('store', 0, 1, 0),
+    ('slopeV', 5),
+    ('sqa', 6),
+    ('whole', 1, 1, 1),
+    ('weave', 4, 0, 2),
+    ('stage1', 0, 7),
+    ('bend', 5),
+    ('store', 2, 1, 1),
+    ('gh0V', 5),
+    ('gh0S', 5),
+    ('gh1', 5),
+    ('slopeV', 6),
+    ('quant_in', 2, 3),
+    ('stage1', 1, 7),
+    ('tanh', 7),
+    ('slopeS', 6),
+    ('whole', 1, 1, 0),
+    ('store', 1, 1, 0),
+    ('quant', 4, 0, 2),
+    ('whole', 0, 1, 1),
+    ('gh2', 5),
+    ('curve', 6),
+    ('stage1', 2, 6),
+    ('weave', 5, 0, 2),
+    ('gh1', 6),
+    ('store', 0, 1, 1),
+    ('sqa', 7),
+    ('quant', 5, 2, 3),
+    ('quant', 5, 0, 2),
+    ('bend', 6),
+    ('sqt', 7),
+    ('stage1', 2, 7),
+    ('store', 1, 1, 1),
+    ('curve', 7),
+    ('slopeS', 7),
+    ('whole', 2, 2, 0),
+    ('gh2', 6),
+    ('quant', 6, 2, 3),
+    ('store', 2, 2, 0),
+    ('whole', 2, 2, 1),
+    ('slopeV', 7),
+    ('whole', 1, 2, 1),
+    ('weave', 6, 0, 2),
+    ('store', 2, 2, 1),
+    ('gh0V', 7),
+    ('gh0S', 7),
+    ('gh1', 7),
+    ('whole', 1, 2, 0),
+    ('store', 1, 2, 0),
+    ('quant', 6, 0, 2),
+    ('whole', 0, 2, 1),
+    ('store', 0, 2, 1),
+    ('part', 1, 3, 0, 0),
+    ('part', 1, 3, 1, 0),
+    ('weave', 7, 0, 1),
+    ('whole', 0, 2, 0),
+    ('quant', 7, 2, 3),
+    ('store', 1, 2, 1),
+    ('part', 0, 3, 0, 0),
+    ('part', 1, 3, 1, 1),
+    ('bend', 7),
+    ('store', 0, 2, 0),
+    ('part', 0, 3, 1, 0),
+    ('part', 1, 3, 0, 1),
+    ('quant', 7, 0, 1),
+    ('part', 0, 3, 1, 1),
+    ('gh2', 7),
+    ('store', 1, 3, 1),
+    ('store', 1, 3, 0),
+    ('store', 0, 3, 1),
+    ('part', 2, 3, 0, 0),
+    ('weave', 7, 1, 2),
+    ('part', 0, 3, 0, 1),
+    ('quant', 7, 1, 2),
+    ('part', 2, 3, 1, 0),
+    ('store', 0, 3, 0),
+    ('part', 2, 3, 0, 1),
+    ('part', 2, 3, 1, 1),
+    ('store', 2, 3, 0),
+    ('store', 2, 3, 1),
+)
+GH0_S = (0, 3, 2, 3, 4, 3, 2, 4)
 FLOPS = 6 * 2 * B * D * H
 
 
@@ -65,13 +322,12 @@ def tile_taylormodesecondordertanhjet_d2p_kernel(tc, x_bytes, x_scale, v, q, w1_
         def widen(i):
             st["xw", i] = work.tile([P, D], BF16, name="xw", tag="xw", align_bytes=64)
             for j in range(8):
-                nc.vector.tensor_scalar(
-                    out=st["xw", i][:, P * j : P * (j + 1)],
-                    in0=x_u8[:, i, P * j : P * (j + 1)].bitcast(F8),
-                    scalar1=xs[:, 8 * i + j : 8 * i + j + 1],
-                    scalar2=None,
-                    op0=ALU.mult,
-                )
+                block = slice(P * j, P * (j + 1))
+                scale = xs[:, 8 * i + j : 8 * i + j + 1]
+                if j < WIDEN_S[i]:
+                    nc.scalar.activation(out=st["xw", i][:, block], in_=x_u8[:, i, block].bitcast(F8), func=ACT.Copy, scale=scale)
+                else:
+                    nc.vector.tensor_scalar(out=st["xw", i][:, block], in0=x_u8[:, i, block].bitcast(F8), scalar1=scale, scalar2=None, op0=ALU.mult)
 
         def flip(o, i):
             rows = st["xw", i] if o == 0 else raw[o, i]
@@ -88,8 +344,8 @@ def tile_taylormodesecondordertanhjet_d2p_kernel(tc, x_bytes, x_scale, v, q, w1_
             st["xg", o, i] = xg
 
         def quant_in(o, i):
-            xc = work.tile([P, 256], U32, name="xc%d" % o, tag="xc%d" % o, align_bytes=64)
-            xq = work.tile([P, 256], U8, name="xq%d" % o, tag="xq%d" % o, align_bytes=64)
+            xc = work.tile([P, 256], U32, name="xc%d" % o, tag="xc%d" % o, bufs=3, align_bytes=64)
+            xq = work.tile([P, 256], U8, name="xq%d" % o, tag="xq%d" % o, bufs=3, align_bytes=64)
             nc.vector.quantize_mx(out=xc[:].bitcast(FP8X4), scales=xq[:], in_=st["xg", o, i][:].rearrange("p k r t -> p (k r t)"))
             st["xc", o, i] = (xc, xq)
 
@@ -127,37 +383,42 @@ def tile_taylormodesecondordertanhjet_d2p_kernel(tc, x_bytes, x_scale, v, q, w1_
             nc.scalar.activation(out=sq[:], in_=st["tt", n][:], func=ACT.Square)
             st["sq", n] = sq
 
-        def slope(n, engine_slots):
+        def slope(n, slots, scalar):
             h = n % 2
             if ("gs", n) not in st:
                 st["gs", n] = work.tile([P, 4, P], F32, name="gs", tag="gs")
-            gs = st["gs", n]
-            for t in engine_slots:
+            for t in slots:
                 c0 = 4 * h + t
-                if t < SLOPE_S[n]:
-                    nc.scalar.activation(out=gs[:, t, :], in_=st["sq", n][:, t, :], func=ACT.Identity, bias=g_col[:, c0 : c0 + 1], scale=ng_col[:, c0 : c0 + 1])
-                    continue
-                nc.vector.tensor_scalar(out=gs[:, t, :], in0=st["sq", n][:, t, :], scalar1=ng_col[:, c0 : c0 + 1], scalar2=g_col[:, c0 : c0 + 1], op0=ALU.mult, op1=ALU.add)
+                out, sq = st["gs", n][:, t, :], st["sq", n][:, t, :]
+                gain, minus = g_col[:, c0 : c0 + 1], ng_col[:, c0 : c0 + 1]
+                if scalar:
+                    nc.scalar.activation(out=out, in_=sq, func=ACT.Identity, bias=gain, scale=minus)
+                else:
+                    nc.vector.tensor_scalar(out=out, in0=sq, scalar1=minus, scalar2=gain, op0=ALU.mult, op1=ALU.add)
 
         def curve(n):
             w = work.tile([P, 4, P], F32, name="w", tag="w")
             nc.vector.scalar_tensor_tensor(out=w[:], in0=st["tt", n][:], scalar=-2.0, in1=st["c", n][:], op0=ALU.mult, op1=ALU.mult)
             st["w", n] = w
 
-        def gh0(n, slots):
+        def gh0(n, slots, scalar):
             h = n % 2
             if ("hb", n) not in st:
                 st["hb", n] = work.tile([P, 2, 4, P], BF16, name="hb", tag="hb", align_bytes=64)
             for t in slots:
                 gain = g_col[:, 4 * h + t : 4 * h + t + 1]
-                if t < GH0_S[n]:
+                if scalar:
                     nc.scalar.activation(out=st["hb", n][:, 0, t, :], in_=st["tt", n][:, t, :], func=ACT.Copy, scale=gain)
                 else:
                     nc.vector.tensor_scalar(out=st["hb", n][:, 0, t, :], in0=st["tt", n][:, t, :], scalar1=gain, scalar2=None, op0=ALU.mult)
 
+        def woven(n):
+            if ("hq", n) not in st:
+                st["hq", n] = work.tile([P, 3, P, 4], BF16, name="hq", tag="hq", align_bytes=64)
+            return st["hq", n]
+
         def gh1(n):
-            st["hq", n] = work.tile([P, 3, P, 4], BF16, name="hq", tag="hq", align_bytes=64)
-            nc.vector.tensor_tensor(out=st["hq", n][:, 2, :, :], in0=st["gs", n][:].rearrange("p t n -> p n t"), in1=st["a", 1, n][:].rearrange("p t n -> p n t"), op=ALU.mult)
+            nc.vector.tensor_tensor(out=woven(n)[:, 2, :, :], in0=st["gs", n][:].rearrange("p t n -> p n t"), in1=st["a", 1, n][:].rearrange("p t n -> p n t"), op=ALU.mult)
 
         def bend(n):
             e = work.tile([P, 4, P], F32, name="e", tag="e")
@@ -167,15 +428,17 @@ def tile_taylormodesecondordertanhjet_d2p_kernel(tc, x_bytes, x_scale, v, q, w1_
         def gh2(n):
             nc.vector.tensor_tensor(out=st["hb", n][:, 1, :, :], in0=st["gs", n][:], in1=st["e", n][:], op=ALU.mult)
 
-        def weave(n, lo, hi):
+        def weave(n, lo, hi, copy=nc.vector.tensor_copy):
             s = slice(lo, hi)
-            nc.vector.tensor_copy(out=st["hq", n][:, s, :, :].rearrange("p o (c i) t -> p o c t i", i=4), in_=st["hb", n][:, s, :, :].rearrange("p o t (c i) -> p o c t i", i=4))
+            copy(out=woven(n)[:, s, :, :].rearrange("p o (c i) t -> p o c t i", i=4), in_=st["hb", n][:, s, :, :].rearrange("p o t (c i) -> p o c t i", i=4))
 
         def codes(n):
             st["hc", n] = work.tile([P, 3 * P], U32, name="hc", tag="hc", bufs=4, align_bytes=64)
             st["hs", n] = work.tile([P, 3 * P], U8, name="hs", tag="hs", bufs=4, align_bytes=64)
 
         def quant(n, lo, hi):
+            if ("hc", n) not in st:
+                codes(n)
             nc.vector.quantize_mx(
                 out=st["hc", n][:, P * lo : P * hi].bitcast(FP8X4),
                 scales=st["hs", n][:, P * lo : P * hi],
@@ -199,7 +462,8 @@ def tile_taylormodesecondordertanhjet_d2p_kernel(tc, x_bytes, x_scale, v, q, w1_
                     stop=(k == 1),
                 )
 
-        def store(o, i, half, on_vector=False):
+        def store(o, i, half):
+            on_vector = Y_V[6 * i + 2 * (1, 0, 2)[o] + half]
             y_sb = work.tile([P, 512], F32, name="y_sb", tag="y_sb", bufs=12)
             if on_vector:
                 nc.vector.tensor_copy(out=y_sb[:], in_=st["y", o, i, half][:])
@@ -207,10 +471,7 @@ def tile_taylormodesecondordertanhjet_d2p_kernel(tc, x_bytes, x_scale, v, q, w1_
                 nc.scalar.copy(out=y_sb[:], in_=st["y", o, i, half][:])
             nc.sync.dma_start(out=outs[o][P * i : P * (i + 1), 512 * half : 512 * (half + 1)], in_=y_sb[:])
 
-        pieces = [(o, half) for o in (1, 0, 2) for half in range(2)]
-
         with tc.manual_schedule():
-            waiting = []
             nc.vector.memset(s1_raw[:].bitcast(I32), 0)
             nc.vector.memset(s2[:].bitcast(I32), 0)
             nc.gpsimd.dma_start(out=b_col[:].rearrange("p (k t) -> p k t", k=2), in_=b.rearrange("(k p t) -> p k t", k=2, t=4))
@@ -218,22 +479,25 @@ def tile_taylormodesecondordertanhjet_d2p_kernel(tc, x_bytes, x_scale, v, q, w1_
             make_identity(nc, ident[:])
             nc.gpsimd.tensor_copy(out=g_col[:], in_=g_raw[:])
             nc.gpsimd.tensor_scalar(out=ng_col[:], in0=g_col[:], scalar1=-1.0, scalar2=None, op0=ALU.mult)
-            load_rows(1, 0)
-            nc.scalar.dma_start(out=xs[:], in_=x_scale.rearrange("i j -> (i j)").partition_broadcast(P))
-            nc.sync.dma_start(out=x_u8[:, 0, :], in_=x_bytes[0:P, :])
-            load_scales(s1_raw, w1_scales, nc.scalar)
-            load_w1(0)
-            load_rows(2, 0)
-            nc.sync.dma_start(out=x_u8[:, 1, :], in_=x_bytes[P : 2 * P, :])
-            load_w1(1)
-            load_rows(1, 1)
-            load_rows(2, 1)
-            nc.sync.dma_start(out=x_u8[:, 2:TILES, :], in_=x_bytes[2 * P : B, :].rearrange("(i p) k -> p i k", p=P))
-            nc.sync.dma_start(out=w2[:], in_=w2_words.rearrange("g p n t -> p g (n t)").bitcast(I32))
-            load_scales(s2, w2_scales, nc.sync)
-            for i in (2, 3):
-                load_rows(1, i)
-                load_rows(2, i)
+            def load(what):
+                if what == "xs":
+                    nc.scalar.dma_start(out=xs[:], in_=x_scale.rearrange("i j -> (i j)").partition_broadcast(P))
+                elif what == "s1":
+                    load_scales(s1_raw, w1_scales, nc.scalar)
+                elif what == "x0":
+                    nc.sync.dma_start(out=x_u8[:, 0, :], in_=x_bytes[0:P, :])
+                elif what == "x1":
+                    nc.sync.dma_start(out=x_u8[:, 1, :], in_=x_bytes[P : 2 * P, :])
+                elif what == "x23":
+                    nc.sync.dma_start(out=x_u8[:, 2:TILES, :], in_=x_bytes[2 * P : B, :].rearrange("(i p) k -> p i k", p=P))
+                elif what == "w2":
+                    nc.sync.dma_start(out=w2[:], in_=w2_words.rearrange("g p n t -> p g (n t)").bitcast(I32))
+                elif what == "s2":
+                    load_scales(s2, w2_scales, nc.sync)
+                elif what[0] == "w":
+                    load_w1(int(what[2]))
+                else:
+                    load_rows(1 if what[0] == "v" else 2, int(what[1]))
 
             def permute_words(h):
                 nc.vector.tensor_copy(out=w1_per[h][:].rearrange("p k (t m) -> p k t m", t=4), in_=w1_raw[h][:].rearrange("p k (m t) -> p k t m", t=4))
@@ -241,118 +505,46 @@ def tile_taylormodesecondordertanhjet_d2p_kernel(tc, x_bytes, x_scale, v, q, w1_
             def permute_scales(h):
                 nc.vector.tensor_copy(out=s1_per[:, h, :].rearrange("p (t m) -> p t m", t=4), in_=s1_raw[:, 512 * h : 512 * (h + 1)].rearrange("p (m t) -> p t m", t=4))
 
-            flip(1, 0)
-            widen(0)
-            gather(1, 0)
-            flip(0, 0)
-            quant_in(1, 0)
-            gather(0, 0)
-            permute_words(0)
-            permute_scales(0)
-            quant_in(0, 0)
-            stage1(1, 0)
-            stage1(0, 0)
-            square_a1(0)
-            flip(2, 0)
-            tanh(0)
-            gather(2, 0)
-            widen(1)
-            flip(0, 1)
-            square_t(0)
-            permute_words(1)
-            permute_scales(1)
-            quant_in(2, 0)
-            gather(0, 1)
-            stage1(2, 0)
-            slope(0, range(SLOPE_S[0]))
-            gh0(0, range(GH0_S[0]))
+            def last_bank(o, half):
+                tag, bufs = (("a0", 1), ("a1", 2), ("a1", 2), ("a2", 2), ("a2", 2), ("ytr", 3))[2 * (1, 0, 2)[o] + half] if False else LASTB[2 * (1, 0, 2)[o] + half]
+                bank(o, TILES - 1, half, tag, bufs)
 
-            for n in range(UNITS):
-                nxt = n + 1
-                first = n % 2 == 0
-                done = n // 2 - 1
-                ahead = n // 2 + 1
-                late = nxt == UNITS
-                todo = [(o, half) for o, half in (pieces[0:SPLIT[done]] if first else pieces[SPLIT[done]:6]) if done >= 0]
+            def whole(o, i, half):
+                bank(o, i, half)
+                product(o, i, half)
 
-                def make(m):
-                    if m < len(todo):
-                        bank(todo[m][0], done, todo[m][1])
-                        product(todo[m][0], done, todo[m][1])
-                        waiting.append((todo[m][0], done, todo[m][1]))
+            def part(o, i, half, k):
+                if k == 0:
+                    last_bank(o, half)
+                product(o, i, half, (k,))
 
-                def drain():
-                    if waiting:
-                        store(*waiting.pop(0))
+            def run(key):
+                a = key[1:]
+                what = key[0]
+                if what == "load": load(*a)
+                elif what == "widen": widen(*a)
+                elif what == "flip": flip(*a)
+                elif what == "gather": gather(*a)
+                elif what == "quant_in": quant_in(*a)
+                elif what == "permw": permute_words(*a)
+                elif what == "perms": permute_scales(*a)
+                elif what == "stage1": stage1(*a)
+                elif what == "tanh": tanh(*a)
+                elif what == "sqa": square_a1(*a)
+                elif what == "sqt": square_t(*a)
+                elif what == "slopeS": slope(a[0], range(SLOPE_S[a[0]]), True)
+                elif what == "slopeV": slope(a[0], range(SLOPE_S[a[0]], 4), False)
+                elif what == "gh0S": gh0(a[0], range(GH0_S[a[0]]), True)
+                elif what == "gh0V": gh0(a[0], range(GH0_S[a[0]], 4), False)
+                elif what == "curve": curve(*a)
+                elif what == "bend": bend(*a)
+                elif what == "gh1": gh1(*a)
+                elif what == "gh2": gh2(*a)
+                elif what == "weave": weave(*a)
+                elif what == "quant": quant(*a)
+                elif what == "whole": whole(*a)
+                elif what == "part": part(*a)
+                elif what == "store": store(*a)
 
-                codes(n)
-                curve(n)
-                if not late:
-                    stage1(0, nxt)
-                    stage1(1, nxt)
-                drain()
-                if not first and ahead < TILES:
-                    quant_in(2, ahead)
-                if n > 0:
-                    weave(n - 1, 0, 2)
-                if not first and ahead + 1 < TILES:
-                    widen(ahead + 1)
-                if not late:
-                    tanh(nxt)
-                    square_a1(nxt)
-                make(0)
-                if first and ahead < TILES:
-                    flip(1, ahead)
-                    gather(1, ahead)
-                elif not first and ahead + 1 < TILES:
-                    flip(0, ahead + 1)
-                    gather(0, ahead + 1)
-                drain()
-                slope(n, range(SLOPE_S[n], 4))
-                if late:
-                    gh1(n)
-                    quant(n - 1, 0, 2)
-                    gh0(n, range(GH0_S[n], 4))
-                else:
-                    gh0(n, range(GH0_S[n], 4))
-                    if n > 0:
-                        quant(n - 1, 0, 2)
-                if not late:
-                    square_t(nxt)
-                    stage1(2, nxt)
-                make(1)
-                if first and ahead < TILES:
-                    flip(2, ahead)
-                    gather(2, ahead)
-                    quant_in(0, ahead)
-                bend(n)
-                drain()
-                if not late:
-                    slope(nxt, range(SLOPE_S[nxt]))
-                if not late:
-                    gh1(n)
-                make(2)
-                make(3)
-                drain()
-                if late:
-                    quant(n, 2, 3)
-                    weave(n, 0, 1)
-                else:
-                    gh0(nxt, range(GH0_S[nxt]))
-                gh2(n)
-                if first and ahead < TILES:
-                    quant_in(1, ahead)
-                if not late:
-                    quant(n, 2, 3)
-            last = UNITS - 1
-            i = TILES - 1
-            drain()
-            quant(last, 0, 1)
-            weave(last, 1, 2)
-            quant(last, 1, 2)
-            for (o, half), tag, bufs in zip(pieces, ("a1", "a2", "a0", "a1", "a2", "ytr"), (2, 2, 1, 2, 2, 3)):
-                bank(o, i, half, tag, bufs)
-                product(o, i, half, (0,))
-            for m, (o, half) in enumerate(pieces):
-                product(o, i, half, (1,))
-                store(o, i, half, on_vector=(m in (3, 5)))
+            for key in PROGRAM:
+                run(key)

from contextlib import ExitStack

import concourse.mybir as mybir
from concourse.masks import make_identity

F32 = mybir.dt.float32
BF16 = mybir.dt.bfloat16
I32 = mybir.dt.int32
U32 = mybir.dt.uint32
U8 = mybir.dt.uint8
F8 = mybir.dt.float8_e4m3fn
FP8X4 = mybir.dt.float8_e4m3fn_x4
ALU = mybir.AluOpType
ACT = mybir.ActivationFunctionType

P = 128
B, D, H, N_OUT = 512, 1024, 1024, 1024
TILES = B // P
UNITS = 2 * TILES
SLOPE_S = (0, 4, 1, 1, 2, 0, 2, 1)
WIDEN_S = (0, 0, 0, 0)
Y_V = (0, 0, 0, 0, 0, 0, 0, 0, 0, 0, 0, 0, 0, 0, 0, 0, 0, 0, 0, 0, 1, 0, 0, 0)
LASTB = (("a1", 2), ("a2", 2), ("a0", 1), ("a1", 2), ("a2", 2), ("ytr", 3))
PROGRAM = (
    ('load', 'xs'),
    ('load', 'x0'),
    ('load', 'v0'),
    ('load', 's1'),
    ('load', 'w10'),
    ('load', 'x1'),
    ('load', 'x23'),
    ('load', 'q0'),
    ('load', 'w11'),
    ('load', 'v1'),
    ('load', 'q1'),
    ('load', 'w2'),
    ('load', 's2'),
    ('load', 'q2'),
    ('load', 'q3'),
    ('load', 'v2'),
    ('load', 'v3'),
    ('widen', 0),
    ('flip', 0, 0),
    ('flip', 1, 0),
    ('perms', 1),
    ('perms', 0),
    ('gather', 0, 0),
    ('gather', 1, 0),
    ('permw', 0),
    ('quant_in', 0, 0),
    ('quant_in', 1, 0),
    ('stage1', 0, 0),
    ('tanh', 0),
    ('widen', 1),
    ('widen', 3),
    ('flip', 0, 1),
    ('widen', 2),
    ('sqt', 0),
    ('flip', 2, 0),
    ('stage1', 1, 0),
    ('gather', 0, 1),
    ('flip', 1, 1),
    ('permw', 1),
    ('slopeS', 0),
    ('gather', 2, 0),
    ('gh0S', 0),
    ('gh0V', 0),
    ('sqa', 0),
    ('stage1', 0, 1),
    ('gather', 1, 1),
    ('quant_in', 0, 1),
    ('slopeV', 0),
    ('quant_in', 2, 0),
    ('stage1', 1, 1),
    ('tanh', 1),
    ('curve', 0),
    ('stage1', 2, 0),
    ('quant_in', 1, 1),
    ('stage1', 0, 2),
    ('gh1', 0),
    ('flip', 2, 1),
    ('sqa', 1),
    ('bend', 0),
    ('flip', 0, 2),
    ('sqt', 1),
    ('stage1', 2, 1),
    ('tanh', 2),
    ('curve', 1),
    ('slopeS', 1),
    ('gather', 2, 1),
    ('gather', 0, 2),
    ('gh2', 0),
    ('sqt', 2),
    ('stage1', 1, 2),
    ('quant', 0, 2, 3),
    ('gh0S', 2),
    ('flip', 1, 2),
    ('gh0V', 2),
    ('slopeV', 1),
    ('sqa', 2),
    ('weave', 0, 0, 2),
    ('stage1', 0, 3),
    ('gather', 1, 2),
    ('bend', 1),
    ('gh0V', 1),
    ('gh0S', 1),
    ('gh1', 1),
    ('quant_in', 0, 2),
    ('slopeV', 2),
    ('quant_in', 2, 1),
    ('stage1', 1, 3),
    ('tanh', 3),
    ('slopeS', 2),
    ('quant', 0, 0, 2),
    ('gh2', 1),
    ('curve', 2),
    ('stage1', 2, 2),
    ('weave', 1, 0, 2),
    ('quant_in', 1, 2),
    ('stage1', 0, 4),
    ('gh1', 2),
    ('flip', 2, 2),
    ('sqa', 3),
    ('quant', 1, 2, 3),
    ('quant', 1, 0, 2),
    ('bend', 2),
    ('flip', 0, 3),
    ('sqt', 3),
    ('stage1', 2, 3),
    ('tanh', 4),
    ('curve', 3),
    ('slopeS', 3),
    ('gather', 2, 2),
    ('whole', 2, 0, 0),
    ('gather', 0, 3),
    ('gh2', 2),
    ('sqt', 4),
    ('stage1', 1, 4),
    ('whole', 0, 0, 0),
    ('quant', 2, 2, 3),
    ('gh0S', 4),
    ('store', 2, 0, 0),
    ('flip', 1, 3),
    ('gh0V', 4),
    ('whole', 2, 0, 1),
    ('store', 0, 0, 0),
    ('slopeV', 3),
    ('sqa', 4),
    ('whole', 1, 0, 1),
    ('weave', 2, 0, 2),
    ('stage1', 0, 5),
    ('gather', 1, 3),
    ('bend', 3),
    ('store', 2, 0, 1),
    ('gh0V', 3),
    ('gh0S', 3),
    ('gh1', 3),
    ('quant_in', 0, 3),
    ('slopeV', 4),
    ('quant_in', 2, 2),
    ('stage1', 1, 5),
    ('tanh', 5),
    ('slopeS', 4),
    ('whole', 1, 0, 0),
    ('store', 1, 0, 0),
    ('quant', 2, 0, 2),
    ('whole', 0, 0, 1),
    ('gh2', 3),
    ('curve', 4),
    ('stage1', 2, 4),
    ('weave', 3, 0, 2),
    ('quant_in', 1, 3),
    ('stage1', 0, 6),
    ('gh1', 4),
    ('store', 0, 0, 1),
    ('flip', 2, 3),
    ('sqa', 5),
    ('quant', 3, 2, 3),
    ('quant', 3, 0, 2),
    ('bend', 4),
    ('sqt', 5),
    ('stage1', 2, 5),
    ('tanh', 6),
    ('store', 1, 0, 1),
    ('curve', 5),
    ('slopeS', 5),
    ('gather', 2, 3),
    ('whole', 2, 1, 0),
    ('gh2', 4),
    ('sqt', 6),
    ('stage1', 1, 6),
    ('whole', 0, 1, 0),
    ('quant', 4, 2, 3),
    ('gh0S', 6),
    ('store', 2, 1, 0),
    ('gh0V', 6),
    ('whole', 2, 1, 1),
    ('store', 0, 1, 0),
    ('slopeV', 5),
    ('sqa', 6),
    ('whole', 1, 1, 1),
    ('weave', 4, 0, 2),
    ('stage1', 0, 7),
    ('bend', 5),
    ('store', 2, 1, 1),
    ('gh0V', 5),
    ('gh0S', 5),
    ('gh1', 5),
    ('slopeV', 6),
    ('quant_in', 2, 3),
    ('stage1', 1, 7),
    ('tanh', 7),
    ('slopeS', 6),
    ('whole', 1, 1, 0),
    ('store', 1, 1, 0),
    ('quant', 4, 0, 2),
    ('whole', 0, 1, 1),
    ('gh2', 5),
    ('curve', 6),
    ('stage1', 2, 6),
    ('weave', 5, 0, 2),
    ('gh1', 6),
    ('store', 0, 1, 1),
    ('sqa', 7),
    ('quant', 5, 2, 3),
    ('quant', 5, 0, 2),
    ('bend', 6),
    ('sqt', 7),
    ('stage1', 2, 7),
    ('store', 1, 1, 1),
    ('curve', 7),
    ('slopeS', 7),
    ('whole', 2, 2, 0),
    ('gh2', 6),
    ('quant', 6, 2, 3),
    ('store', 2, 2, 0),
    ('whole', 2, 2, 1),
    ('slopeV', 7),
    ('whole', 1, 2, 1),
    ('weave', 6, 0, 2),
    ('store', 2, 2, 1),
    ('gh0V', 7),
    ('gh0S', 7),
    ('gh1', 7),
    ('whole', 1, 2, 0),
    ('store', 1, 2, 0),
    ('quant', 6, 0, 2),
    ('whole', 0, 2, 1),
    ('store', 0, 2, 1),
    ('part', 1, 3, 0, 0),
    ('part', 1, 3, 1, 0),
    ('weave', 7, 0, 1),
    ('whole', 0, 2, 0),
    ('quant', 7, 2, 3),
    ('store', 1, 2, 1),
    ('part', 0, 3, 0, 0),
    ('part', 1, 3, 1, 1),
    ('bend', 7),
    ('store', 0, 2, 0),
    ('part', 0, 3, 1, 0),
    ('part', 1, 3, 0, 1),
    ('quant', 7, 0, 1),
    ('part', 0, 3, 1, 1),
    ('gh2', 7),
    ('store', 1, 3, 1),
    ('store', 1, 3, 0),
    ('store', 0, 3, 1),
    ('part', 2, 3, 0, 0),
    ('weave', 7, 1, 2),
    ('part', 0, 3, 0, 1),
    ('quant', 7, 1, 2),
    ('part', 2, 3, 1, 0),
    ('store', 0, 3, 0),
    ('part', 2, 3, 0, 1),
    ('part', 2, 3, 1, 1),
    ('store', 2, 3, 0),
    ('store', 2, 3, 1),
)
GH0_S = (0, 3, 2, 3, 4, 3, 2, 4)
FLOPS = 6 * 2 * B * D * H


def tile_taylormodesecondordertanhjet_d2p_kernel(tc, x_bytes, x_scale, v, q, w1_words, w1_scales, b, g, w2_words, w2_scales, out_0, out_1, out_2):
    nc = tc.nc
    outs = (out_0, out_1, out_2)
    with ExitStack() as ctx:
        keep = ctx.enter_context(tc.tile_pool(name="keep", bufs=1))
        pin = ctx.enter_context(tc.tile_pool(name="pin", bufs=1))
        work = ctx.enter_context(tc.tile_pool(name="work", bufs=2))
        psum = ctx.enter_context(tc.psum_pool(name="psum", bufs=1))

        ident = keep.tile([P, P], F32, name="ident")
        xs = keep.tile([P, 32], F32, name="xs")
        b_col = keep.tile([P, 8], BF16, name="b_col")
        g_raw = keep.tile([P, 8], BF16, name="g_raw")
        g_col = keep.tile([P, 8], F32, name="g_col")
        ng_col = keep.tile([P, 8], F32, name="ng_col")
        x_u8 = keep.tile([P, TILES, D], U8, name="x_u8", align_bytes=64)
        s1_raw = keep.tile([P, H], U8, name="s1_raw", align_bytes=64)
        s2 = keep.tile([P, N_OUT], U8, name="s2", align_bytes=64)
        w1_raw = [keep.tile([P, 2, 512], I32, name="w1_raw%d" % h, align_bytes=64) for h in range(2)]
        w1_per = [keep.tile([P, 2, 512], I32, name="w1_per%d" % h, align_bytes=64) for h in range(2)]
        s1_per = keep.tile([P, 2, 512], U8, name="s1_per", align_bytes=64)
        w2 = keep.tile([P, 2, N_OUT], I32, name="w2", align_bytes=64)
        raw = {}
        for o in (1, 2):
            for i in range(TILES):
                raw[o, i] = pin.tile([P, D], BF16, name="raw%d_%d" % (o, i), align_bytes=64)

        st = {}

        def load_rows(o, i):
            nc.sync.dma_start(out=raw[o, i][:], in_=(v, q)[o - 1][P * i : P * (i + 1), :])

        def load_w1(h):
            nc.sync.dma_start(out=w1_raw[h][:], in_=w1_words[:, :, 512 * h : 512 * (h + 1), :].rearrange("g p n t -> p g (n t)").bitcast(I32))

        def load_scales(dst, src, eng):
            for quad in range(4):
                eng.dma_start(out=dst[32 * quad : 32 * quad + 8, :].bitcast(I32), in_=src[:, 4 * quad : 4 * quad + 4, :].bitcast(I32))

        def widen(i):
            st["xw", i] = work.tile([P, D], BF16, name="xw", tag="xw", align_bytes=64)
            for j in range(8):
                block = slice(P * j, P * (j + 1))
                scale = xs[:, 8 * i + j : 8 * i + j + 1]
                if j < WIDEN_S[i]:
                    nc.scalar.activation(out=st["xw", i][:, block], in_=x_u8[:, i, block].bitcast(F8), func=ACT.Copy, scale=scale)
                else:
                    nc.vector.tensor_scalar(out=st["xw", i][:, block], in0=x_u8[:, i, block].bitcast(F8), scalar1=scale, scalar2=None, op0=ALU.mult)

        def flip(o, i):
            rows = st["xw", i] if o == 0 else raw[o, i]
            words = rows[:].bitcast(F32)
            tr = psum.tile([P, 4, P], F32, name="tr", tag="ytr", bufs=3)
            for k in range(2):
                for u in range(2):
                    nc.tensor.transpose(tr[:, 2 * k + u, :], words[:, 256 * k + u : 256 * (k + 1) : 2], ident[:])
            st["tr", o, i] = tr

        def gather(o, i):
            xg = work.tile([P, 2, P, 4], BF16, name="xg", tag="xg", bufs=3, align_bytes=64)
            nc.scalar.copy(out=xg[:].rearrange("p k r t -> p (k r t)").bitcast(F32).rearrange("p (k r u) -> p k r u", k=2, u=2), in_=st["tr", o, i][:].rearrange("p (k u) r -> p k r u", u=2))
            st["xg", o, i] = xg

        def quant_in(o, i):
            xc = work.tile([P, 256], U32, name="xc%d" % o, tag="xc%d" % o, bufs=3, align_bytes=64)
            xq = work.tile([P, 256], U8, name="xq%d" % o, tag="xq%d" % o, bufs=3, align_bytes=64)
            nc.vector.quantize_mx(out=xc[:].bitcast(FP8X4), scales=xq[:], in_=st["xg", o, i][:].rearrange("p k r t -> p (k r t)"))
            st["xc", o, i] = (xc, xq)

        def stage1(o, n):
            i, h = n // 2, n % 2
            xc, xq = st["xc", o, i]
            a = psum.tile([P, 4, P], F32, name="a%d" % o, tag="a%d" % o, bufs=(1, 2, 2)[o])
            for t in range(4):
                for k in range(2):
                    nc.tensor.matmul_mx(
                        out=a[:, t, :],
                        lhsT=w1_per[h][:, k, P * t : P * (t + 1)].bitcast(FP8X4),
                        lhsT_scale=s1_per[4 * k : P, h, P * t : P * (t + 1)],
                        rhs=xc[:, P * k : P * (k + 1)].bitcast(FP8X4),
                        rhs_scale=xq[:, P * k : P * (k + 1)],
                        start=(k == 0),
                        stop=(k == 1),
                    )
            st["a", o, n] = a

        def tanh(n):
            h = n % 2
            tt = work.tile([P, 4, P], F32, name="tt", tag="tt")
            for t in range(4):
                nc.scalar.activation(out=tt[:, t, :], in_=st["a", 0, n][:, t, :], func=ACT.Tanh, bias=b_col[:, 4 * h + t : 4 * h + t + 1], scale=1.0)
            st["tt", n] = tt

        def square_a1(n):
            c = work.tile([P, 4, P], F32, name="c", tag="c")
            nc.scalar.activation(out=c[:], in_=st["a", 1, n][:], func=ACT.Square)
            st["c", n] = c

        def square_t(n):
            sq = work.tile([P, 4, P], F32, name="sq", tag="sq")
            nc.scalar.activation(out=sq[:], in_=st["tt", n][:], func=ACT.Square)
            st["sq", n] = sq

        def slope(n, slots, scalar):
            h = n % 2
            if ("gs", n) not in st:
                st["gs", n] = work.tile([P, 4, P], F32, name="gs", tag="gs")
            for t in slots:
                c0 = 4 * h + t
                out, sq = st["gs", n][:, t, :], st["sq", n][:, t, :]
                gain, minus = g_col[:, c0 : c0 + 1], ng_col[:, c0 : c0 + 1]
                if scalar:
                    nc.scalar.activation(out=out, in_=sq, func=ACT.Identity, bias=gain, scale=minus)
                else:
                    nc.vector.tensor_scalar(out=out, in0=sq, scalar1=minus, scalar2=gain, op0=ALU.mult, op1=ALU.add)

        def curve(n):
            w = work.tile([P, 4, P], F32, name="w", tag="w")
            nc.vector.scalar_tensor_tensor(out=w[:], in0=st["tt", n][:], scalar=-2.0, in1=st["c", n][:], op0=ALU.mult, op1=ALU.mult)
            st["w", n] = w

        def gh0(n, slots, scalar):
            h = n % 2
            if ("hb", n) not in st:
                st["hb", n] = work.tile([P, 2, 4, P], BF16, name="hb", tag="hb", align_bytes=64)
            for t in slots:
                gain = g_col[:, 4 * h + t : 4 * h + t + 1]
                if scalar:
                    nc.scalar.activation(out=st["hb", n][:, 0, t, :], in_=st["tt", n][:, t, :], func=ACT.Copy, scale=gain)
                else:
                    nc.vector.tensor_scalar(out=st["hb", n][:, 0, t, :], in0=st["tt", n][:, t, :], scalar1=gain, scalar2=None, op0=ALU.mult)

        def woven(n):
            if ("hq", n) not in st:
                st["hq", n] = work.tile([P, 3, P, 4], BF16, name="hq", tag="hq", align_bytes=64)
            return st["hq", n]

        def gh1(n):
            nc.vector.tensor_tensor(out=woven(n)[:, 2, :, :], in0=st["gs", n][:].rearrange("p t n -> p n t"), in1=st["a", 1, n][:].rearrange("p t n -> p n t"), op=ALU.mult)

        def bend(n):
            e = work.tile([P, 4, P], F32, name="e", tag="e")
            nc.vector.tensor_tensor(out=e[:], in0=st["w", n][:], in1=st["a", 2, n][:], op=ALU.add)
            st["e", n] = e

        def gh2(n):
            nc.vector.tensor_tensor(out=st["hb", n][:, 1, :, :], in0=st["gs", n][:], in1=st["e", n][:], op=ALU.mult)

        def weave(n, lo, hi, copy=nc.vector.tensor_copy):
            s = slice(lo, hi)
            copy(out=woven(n)[:, s, :, :].rearrange("p o (c i) t -> p o c t i", i=4), in_=st["hb", n][:, s, :, :].rearrange("p o t (c i) -> p o c t i", i=4))

        def codes(n):
            st["hc", n] = work.tile([P, 3 * P], U32, name="hc", tag="hc", bufs=4, align_bytes=64)
            st["hs", n] = work.tile([P, 3 * P], U8, name="hs", tag="hs", bufs=4, align_bytes=64)

        def quant(n, lo, hi):
            if ("hc", n) not in st:
                codes(n)
            nc.vector.quantize_mx(
                out=st["hc", n][:, P * lo : P * hi].bitcast(FP8X4),
                scales=st["hs", n][:, P * lo : P * hi],
                in_=st["hq", n][:, lo:hi, :, :].rearrange("p o n t -> p (o n t)"),
            )

        def bank(o, i, half, tag="ytr", bufs=3):
            st["y", o, i, half] = psum.tile([P, 512], F32, name="y", tag=tag, bufs=bufs)

        def product(o, i, half, passes=(0, 1)):
            slot = (0, 2, 1)[o]
            for k in passes:
                n = 2 * i + k
                nc.tensor.matmul_mx(
                    out=st["y", o, i, half][:],
                    lhsT=st["hc", n][:, P * slot : P * (slot + 1)].bitcast(FP8X4),
                    lhsT_scale=st["hs", n][:, P * slot : P * (slot + 1)],
                    rhs=w2[:, k, 512 * half : 512 * (half + 1)].bitcast(FP8X4),
                    rhs_scale=s2[4 * k : P, 512 * half : 512 * (half + 1)],
                    start=(k == 0),
                    stop=(k == 1),
                )

        def store(o, i, half):
            on_vector = Y_V[6 * i + 2 * (1, 0, 2)[o] + half]
            y_sb = work.tile([P, 512], F32, name="y_sb", tag="y_sb", bufs=12)
            if on_vector:
                nc.vector.tensor_copy(out=y_sb[:], in_=st["y", o, i, half][:])
            else:
                nc.scalar.copy(out=y_sb[:], in_=st["y", o, i, half][:])
            nc.sync.dma_start(out=outs[o][P * i : P * (i + 1), 512 * half : 512 * (half + 1)], in_=y_sb[:])

        with tc.manual_schedule():
            nc.vector.memset(s1_raw[:].bitcast(I32), 0)
            nc.vector.memset(s2[:].bitcast(I32), 0)
            nc.gpsimd.dma_start(out=b_col[:].rearrange("p (k t) -> p k t", k=2), in_=b.rearrange("(k p t) -> p k t", k=2, t=4))
            nc.gpsimd.dma_start(out=g_raw[:].rearrange("p (k t) -> p k t", k=2), in_=g.rearrange("(k p t) -> p k t", k=2, t=4))
            make_identity(nc, ident[:])
            nc.gpsimd.tensor_copy(out=g_col[:], in_=g_raw[:])
            nc.gpsimd.tensor_scalar(out=ng_col[:], in0=g_col[:], scalar1=-1.0, scalar2=None, op0=ALU.mult)
            def load(what):
                if what == "xs":
                    nc.scalar.dma_start(out=xs[:], in_=x_scale.rearrange("i j -> (i j)").partition_broadcast(P))
                elif what == "s1":
                    load_scales(s1_raw, w1_scales, nc.scalar)
                elif what == "x0":
                    nc.sync.dma_start(out=x_u8[:, 0, :], in_=x_bytes[0:P, :])
                elif what == "x1":
                    nc.sync.dma_start(out=x_u8[:, 1, :], in_=x_bytes[P : 2 * P, :])
                elif what == "x23":
                    nc.sync.dma_start(out=x_u8[:, 2:TILES, :], in_=x_bytes[2 * P : B, :].rearrange("(i p) k -> p i k", p=P))
                elif what == "w2":
                    nc.sync.dma_start(out=w2[:], in_=w2_words.rearrange("g p n t -> p g (n t)").bitcast(I32))
                elif what == "s2":
                    load_scales(s2, w2_scales, nc.sync)
                elif what[0] == "w":
                    load_w1(int(what[2]))
                else:
                    load_rows(1 if what[0] == "v" else 2, int(what[1]))

            def permute_words(h):
                nc.vector.tensor_copy(out=w1_per[h][:].rearrange("p k (t m) -> p k t m", t=4), in_=w1_raw[h][:].rearrange("p k (m t) -> p k t m", t=4))

            def permute_scales(h):
                nc.vector.tensor_copy(out=s1_per[:, h, :].rearrange("p (t m) -> p t m", t=4), in_=s1_raw[:, 512 * h : 512 * (h + 1)].rearrange("p (m t) -> p t m", t=4))

            def last_bank(o, half):
                tag, bufs = (("a0", 1), ("a1", 2), ("a1", 2), ("a2", 2), ("a2", 2), ("ytr", 3))[2 * (1, 0, 2)[o] + half] if False else LASTB[2 * (1, 0, 2)[o] + half]
                bank(o, TILES - 1, half, tag, bufs)

            def whole(o, i, half):
                bank(o, i, half)
                product(o, i, half)

            def part(o, i, half, k):
                if k == 0:
                    last_bank(o, half)
                product(o, i, half, (k,))

            def run(key):
                a = key[1:]
                what = key[0]
                if what == "load": load(*a)
                elif what == "widen": widen(*a)
                elif what == "flip": flip(*a)
                elif what == "gather": gather(*a)
                elif what == "quant_in": quant_in(*a)
                elif what == "permw": permute_words(*a)
                elif what == "perms": permute_scales(*a)
                elif what == "stage1": stage1(*a)
                elif what == "tanh": tanh(*a)
                elif what == "sqa": square_a1(*a)
                elif what == "sqt": square_t(*a)
                elif what == "slopeS": slope(a[0], range(SLOPE_S[a[0]]), True)
                elif what == "slopeV": slope(a[0], range(SLOPE_S[a[0]], 4), False)
                elif what == "gh0S": gh0(a[0], range(GH0_S[a[0]]), True)
                elif what == "gh0V": gh0(a[0], range(GH0_S[a[0]], 4), False)
                elif what == "curve": curve(*a)
                elif what == "bend": bend(*a)
                elif what == "gh1": gh1(*a)
                elif what == "gh2": gh2(*a)
                elif what == "weave": weave(*a)
                elif what == "quant": quant(*a)
                elif what == "whole": whole(*a)
                elif what == "part": part(*a)
                elif what == "store": store(*a)

            for key in PROGRAM:
                run(key)
